import numpy as np
import ml_dtypes


def mxq(x, axis, fmt="e4m3"):
    dtype, down = {"e4m3": (ml_dtypes.float8_e4m3fn, 7), "e5m2": (ml_dtypes.float8_e5m2, 14)}[fmt]
    v = np.moveaxis(np.asarray(x, np.float32).astype(ml_dtypes.bfloat16).astype(np.float64), axis, -1)
    blocks = v.reshape(v.shape[:-1] + (-1, 32))
    amax = np.abs(blocks).max(-1, keepdims=True)
    byte = np.maximum(np.where(amax > 0, np.frexp(amax)[1] - 1 + 127, 0) - down, 1)
    scale = np.exp2(byte - 127.0)
    codes = (blocks / scale).astype(np.float32).astype(dtype).astype(np.float64)
    return np.moveaxis((codes * scale).reshape(v.shape), -1, axis)


WIDE = False


def mx_kscale(k):
    if not WIDE:
        return np.ones(k)
    levels = np.array([10, -10, 5, -5, 0])
    if k % 512:
        return np.exp2(np.random.permutation(np.resize(levels, k // 32))).repeat(32)
    a = np.empty((k // 512, 16))
    for p in range(k // 512):
        a[p, :8] = np.random.permutation(np.resize(levels, 8))
        for g in range(8):
            far = levels[np.abs(levels - a[p, g]) >= 10]
            a[p, g + 8] = far[np.random.randint(len(far))]
    return np.exp2(a.ravel()).repeat(32)


BF16 = ml_dtypes.bfloat16


def bf(x):
    return np.asarray(x, np.float32).astype(BF16)


def f64(x):
    return np.asarray(x).astype(np.float64)


E2M1 = np.array([0.0, 0.5, 1.0, 1.5, 2.0, 3.0, 4.0, 6.0, -0.0, -0.5, -1.0, -1.5, -2.0, -3.0, -4.0, -6.0])


def pack_weight(w, fmt):
    k, n = w.shape
    w = f64(bf(w)).reshape(k // 32, 32, n)
    amax = np.abs(w).max(1)
    if fmt == "e4m3":
        byte = np.frexp(amax)[1] - 1 + 127 - 7
    else:
        mant, ex = np.frexp(amax / 6.0)
        byte = np.where(mant > 0.5, ex, ex - 1) + 127
    byte = np.clip(np.where(amax > 0, byte, 1), 1, 254)
    scaled = (w * np.exp2(127.0 - byte)[:, None, :]).reshape(k, n).astype(np.float32)
    by_word = np.ascontiguousarray(scaled.reshape(k // 512, 128, 4, n).transpose(0, 1, 3, 2))
    if fmt == "e4m3":
        words = by_word.astype(ml_dtypes.float8_e4m3fn).view(np.uint8)
    else:
        c = by_word.astype(ml_dtypes.float4_e2m1fn).view(np.uint8) & 0xF
        words = c[..., 0::2] | (c[..., 1::2] << 4)
    return np.ascontiguousarray(words), np.ascontiguousarray(byte.astype(np.uint8).reshape(k // 512, 16, n))


def unpack_weight(words, scales, fmt):
    g, p, n, _ = words.shape
    if fmt == "e4m3":
        vals = np.ascontiguousarray(words).view(ml_dtypes.float8_e4m3fn).astype(np.float64)
    else:
        nib = np.empty((g, p, n, 4), np.uint8)
        nib[..., 0::2] = words & 0xF
        nib[..., 1::2] = words >> 4
        vals = E2M1[nib]
    vals = vals * np.repeat(np.exp2(scales.astype(np.float64) - 127.0), 8, axis=1)[..., None]
    return vals.transpose(0, 1, 3, 2).reshape(g * 512, n)
def pack4(w):
    words, scales = pack_weight(w, "e2m1")
    return words.reshape(words.shape[0], 128, -1), scales


def unpack4(words, scales):
    return unpack_weight(words.reshape(words.shape[0], 128, -1, 2), scales, "e2m1")


def planes(Y):
    n, m = Y.shape
    b = f64(bf(Y)).reshape(n // 32, 32, m)
    amax = np.abs(b).max(1)
    byte = np.clip(np.where(amax > 0, np.frexp(amax)[1] - 1 + 127 - 7, 1), 1, 254)
    codes = (b * np.exp2(127.0 - byte)[:, None, :]).reshape(n, m).astype(np.float32).astype(ml_dtypes.float8_e4m3fn).view(np.uint8)
    words = codes.reshape(n // 512, 128, 4, m).transpose(0, 1, 3, 2)
    return np.ascontiguousarray(words), np.ascontiguousarray(byte.astype(np.uint8).reshape(n // 512, 16, m))


N, D, K = 2048, 512, 1024


def softmax_rows(l):
    e = np.exp(l - np.max(l, axis=-1, keepdims=True))
    return e / np.sum(e, axis=-1, keepdims=True)


def setup_inputs():
    s, t, u = mx_kscale(D), mx_kscale(D), mx_kscale(N)
    a = 1.5 / np.sqrt(D)
    x = bf(np.random.standard_normal((N, D)) * s)
    y = bf(np.random.standard_normal((N, D)) / u[:, None])
    eta_words, eta_scales = pack4((a * np.random.standard_normal((K, D)) / s).T)
    dp_words, dp_scales = pack4((a * np.random.standard_normal((K, D)) / t).T)
    return {
        "x": x,
        "y": y,
        "eta_words": eta_words,
        "eta_scales": eta_scales,
        "dp_words": dp_words,
        "dp_scales": dp_scales,
        "g": bf(np.random.standard_normal(D) * t / (s * s)),
        "c": bf(np.random.standard_normal(K)),
        "w": bf(3.0 * np.random.standard_normal(N) * u),
    }


def core(x, y, eta_words, eta_scales, dp_words, dp_scales, g, c, w):
    x, y, g, c, w = f64(x), f64(y), f64(g), f64(c), f64(w)
    q = x * x * g[None, :]
    lin = mxq(x, 1, "e4m3") @ unpack4(eta_words, eta_scales)
    quad = mxq(q, 1, "e4m3") @ unpack4(dp_words, dp_scales)
    l = lin - 0.5 * quad + c[None, :]
    r = softmax_rows(l)
    nk = np.sum(r, axis=0)
    rw = r * w[:, None]
    return (mxq(rw, 0, "e4m3").T @ mxq(y, 0, "e4m3")) / nk[:, None]


def reference(x, y, eta_words, eta_scales, dp_words, dp_scales, g, c, w):
    R_out = core(x, y, eta_words, eta_scales, dp_words, dp_scales, g, c, w)
    words, scales = planes(R_out.T)
    return R_out, words, scales

@@ -1,0 +1,634 @@
+from contextlib import ExitStack
+
+import concourse.mybir as mybir
+from concourse.masks import make_identity
+
+N, D, K = 2048, 512, 1024
+FLOPS = 3 * 2 * N * D * K
+
+F32 = mybir.dt.float32
+BF16 = mybir.dt.bfloat16
+U32 = mybir.dt.uint32
+I32 = mybir.dt.int32
+U8 = mybir.dt.uint8
+FP8X4 = mybir.dt.float8_e4m3fn_x4
+FP4X4 = mybir.dt.float4_e2m1fn_x4
+ALU = mybir.AluOpType
+ACT = mybir.ActivationFunctionType
+
+P = 128
+PACK = 4
+GROUPS = N // (P * PACK)
+TILES = GROUPS * PACK
+BANK = 512
+KT = K // P
+RING = 4
+
+
+def tile_quadraticsoftmaxweightedaverage_kernel(
+    tc, x, y, eta_words, eta_scales, dp_words, dp_scales, g, c, w, out_0, out_1, out_2
+):
+    nc = tc.nc
+    with ExitStack() as ctx:
+        sb = ctx.enter_context(tc.tile_pool(name="sb", bufs=1))
+        ps = ctx.enter_context(tc.psum_pool(name="ps", bufs=1))
+        ctx.enter_context(tc.manual_schedule())
+
+        def sbuf(name, shape, dtype):
+            return sb.tile(shape, dtype, name=name, align_bytes=64)
+
+        banks = [ps.tile([P, BANK], F32, name="bank%d" % b) for b in range(8)]
+        logit_banks = [banks[0:2], banks[2:4]]
+        turn_banks = banks[4:6]
+        nk_bank = banks[6]
+        mean_banks = [banks[b] for b in (7, 4, 5, 0, 1, 2, 3, 6)]
+
+        ident = sbuf("ident", [P, P], F32)
+        minus_ones = sbuf("minus_ones", [P, P], BF16)
+        c_row = sbuf("c_row", [P, K], BF16)
+        minus_c = sbuf("minus_c", [P, K], F32)
+        g_raw = sbuf("g_raw", [P, PACK], BF16)
+        g_half = sbuf("g_half", [P, PACK], F32)
+        w_raw = sbuf("w_raw", [P, GROUPS, PACK], BF16)
+        warm = sbuf("warm", [P, 1], F32)
+        eta_codes = sbuf("eta_codes", [P, 2 * K], U8)
+        dp_codes = sbuf("dp_codes", [P, 2 * K], U8)
+        eta_plane = sbuf("eta_plane", [P, K], U8)
+        dp_plane = sbuf("dp_plane", [P, K], U8)
+        x_raw = [sbuf("x_raw%d" % i, [P, PACK, D], BF16) for i in range(GROUPS)]
+        y_raw = [sbuf("y_raw%d" % i, [P, PACK, D], BF16) for i in range(GROUPS)]
+        xq = [sbuf("xq%d" % i, [P, PACK, 2, P, PACK], BF16) for i in range(2)]
+        sq = [sbuf("sq%d" % i, [P, PACK, P, PACK], F32) for i in range(2)]
+        xq_codes = [sbuf("xq_codes%d" % i, [P, PACK, 2, P], U32) for i in range(GROUPS)]
+        xq_plane = [sbuf("xq_plane%d" % i, [P, PACK, 2, P], U8) for i in range(GROUPS)]
+        y_grouped = [sbuf("y_grouped%d" % i, [P, D, PACK], BF16) for i in range(2)]
+        y_codes = [sbuf("y_codes%d" % i, [P, D], U32) for i in range(GROUPS)]
+        y_plane = [sbuf("y_plane%d" % i, [P, D], U8) for i in range(GROUPS)]
+        neg_logits = [sbuf("neg_logits%d" % i, [P, K], F32) for i in range(3)]
+        expo = sbuf("expo", [P, PACK, K], F32)
+        neg_max = sbuf("neg_max", [P, TILES], F32)
+        row_sum = sbuf("row_sum", [P, TILES], F32)
+        inv_sum = sbuf("inv_sum", [P, TILES], F32)
+        gain = sbuf("gain", [P, TILES], F32)
+        rw_rows = [sbuf("rw_rows%d" % i, [P, PACK, K], BF16) for i in range(2)]
+        rw_grouped = [sbuf("rw_grouped%d" % i, [P, K, PACK], BF16) for i in range(2)]
+        rw_codes = [sbuf("rw_codes%d" % i, [P, K], U32) for i in range(GROUPS)]
+        rw_plane = [sbuf("rw_plane%d" % i, [P, K], U8) for i in range(GROUPS)]
+        nk = sbuf("nk", [P, KT], F32)
+        inv_nk = sbuf("inv_nk", [P, KT], F32)
+        mean = [sbuf("mean%d" % i, [P, D], F32) for i in range(KT)]
+        mean_bf = [sbuf("mean_bf%d" % i, [P, D], BF16) for i in range(RING)]
+        p_grouped = sbuf("p_grouped", [P, K, PACK], BF16)
+        p_codes = sbuf("p_codes", [P, K], U32)
+        p_plane = sbuf("p_plane", [P, K], U8)
+
+        def rows_of(src, gi):
+            return src[P * PACK * gi : P * PACK * (gi + 1), :].rearrange("(p t) d -> p t d", t=PACK)
+
+        def load_plane(plane, scales):
+            for q in range(4):
+                nc.scalar.dma_start(
+                    out=plane[32 * q : 32 * q + 4, :].bitcast(I32), in_=scales[0, 4 * q : 4 * q + 4, :].bitcast(I32)
+                )
+
+        def turn_x(gi, t0, t1):
+            for t in range(t0, t1):
+                words = x_raw[gi][:, t, :].bitcast(F32)
+                for u in range(2):
+                    col = (2 * (t % 2) + u) * P
+                    nc.tensor.transpose(turn_banks[t // 2][:, col : col + P], words[:, u : D // 2 : 2], ident[:])
+
+        def copy_x(on_vector, gi, t0, t1):
+            src = turn_banks[t0 // 2][:].rearrange("p (t u m) -> p t m u", t=2, u=2)[:, t0 % 2 : t0 % 2 + t1 - t0]
+            dst = xq[gi % 2][:, t0:t1, 0].bitcast(F32)
+            if on_vector:
+                nc.vector.tensor_copy(out=dst, in_=src)
+            else:
+                nc.scalar.copy(out=dst, in_=src)
+
+        def square_x(gi, t0, t1):
+            nc.scalar.activation(out=sq[gi % 2][:, t0:t1], in_=xq[gi % 2][:, t0:t1, 0], func=ACT.Square)
+
+        def make_q(engine, gi, t0, t1):
+            (nc.gpsimd if engine == "pool" else nc.vector).tensor_tensor(
+                out=xq[gi % 2][:, t0:t1, 1],
+                in0=sq[gi % 2][:, t0:t1],
+                in1=g_half[:].unsqueeze(1).unsqueeze(1).to_broadcast([P, t1 - t0, P, PACK]),
+                op=ALU.mult,
+            )
+
+        def quantize_xq(gi, t0, t1):
+            nc.vector.quantize_mx(
+                out=xq_codes[gi][:, t0:t1].rearrange("p t s m -> p (t s m)").bitcast(FP8X4),
+                scales=xq_plane[gi][:, t0:t1].rearrange("p t s m -> p (t s m)"),
+                in_=xq[gi % 2][:, t0:t1].rearrange("p t s m j -> p (t s m j)"),
+            )
+
+        def logits(i):
+            gi, t = divmod(i, PACK)
+            for h in range(2):
+                for s, (codes, plane) in enumerate(((eta_codes, eta_plane), (dp_codes, dp_plane))):
+                    nc.tensor.matmul_mx(
+                        out=logit_banks[i % 2][h][:],
+                        lhsT=xq_codes[gi][:, t, s, :].bitcast(FP8X4),
+                        lhsT_scale=xq_plane[gi][:, t, s, :],
+                        rhs=codes[:, 2 * BANK * h : 2 * BANK * (h + 1)].bitcast(FP4X4),
+                        rhs_scale=plane[:, BANK * h : BANK * (h + 1)],
+                        start=(s == 0),
+                        stop=(s == 1),
+                    )
+
+        def add_c(i, h):
+            cols = slice(BANK * h, BANK * (h + 1))
+            nc.vector.tensor_tensor(
+                out=neg_logits[i % 3][:, cols], in0=minus_c[:, cols], in1=logit_banks[i % 2][h][:], op=ALU.subtract
+            )
+
+        def row_max(i):
+            nc.vector.tensor_reduce(
+                out=neg_max[:, i : i + 1], in_=neg_logits[i % 3][:], axis=mybir.AxisListType.X, op=ALU.min
+            )
+
+        def exponent(i):
+            nc.scalar.activation(
+                out=expo[:, i % PACK, :],
+                in_=neg_logits[i % 3][:],
+                func=ACT.Exp,
+                bias=neg_max[:, i : i + 1],
+                scale=-1.0,
+                accum_out=row_sum[:, i : i + 1],
+            )
+
+        def invert_sum(i):
+            nc.vector.reciprocal(out=inv_sum[:, i : i + 1], in_=row_sum[:, i : i + 1])
+
+        def make_gain(i):
+            gi, t = divmod(i, PACK)
+            nc.scalar.activation(
+                out=gain[:, i : i + 1], in_=w_raw[:, gi, t : t + 1], func=ACT.Copy, scale=inv_sum[:, i : i + 1]
+            )
+
+        def weigh(i):
+            gi, t = divmod(i, PACK)
+            nc.scalar.activation(
+                out=rw_rows[gi % 2][:, t, :], in_=expo[:, t, :], func=ACT.Copy, scale=gain[:, i : i + 1]
+            )
+
+        def weigh_grouped(gi, k0, k1):
+            nc.vector.tensor_tensor(
+                out=rw_grouped[gi % 2][:, k0:k1, :].rearrange("p (c i) t -> p c t i", i=PACK),
+                in0=expo[:, :, k0:k1].rearrange("p t (c i) -> p c t i", i=PACK),
+                in1=gain[:, PACK * gi : PACK * (gi + 1)].unsqueeze(1).unsqueeze(3).to_broadcast([P, (k1 - k0) // PACK, PACK, PACK]),
+                op=ALU.mult,
+            )
+
+        def column_sums(i):
+            for kt in range(KT):
+                col = kt * TILES + i
+                nc.tensor.matmul(
+                    out=nk_bank[:, col : col + 1],
+                    lhsT=expo[:, i % PACK, P * kt : P * (kt + 1)],
+                    rhs=inv_sum[:, i : i + 1],
+                    start=True,
+                    stop=True,
+                )
+
+        def interleave(engine, dst, src):
+            src = src.rearrange("p t n -> p n t")
+            if engine == "pool":
+                nc.gpsimd.tensor_scalar(out=dst, in0=src, scalar1=1.0, scalar2=0.0, op0=ALU.mult, op1=ALU.add)
+            elif engine == "scalar":
+                nc.scalar.copy(out=dst, in_=src)
+            else:
+                nc.vector.tensor_copy(out=dst, in_=src)
+
+        def group_rw(engine, gi, k0, k1):
+            interleave(engine, rw_grouped[gi % 2][:, k0:k1, :], rw_rows[gi % 2][:, :, k0:k1])
+
+        def quantize_rw(gi, k0, k1):
+            nc.vector.quantize_mx(
+                out=rw_codes[gi][:, k0:k1].bitcast(FP8X4),
+                scales=rw_plane[gi][:, k0:k1],
+                in_=rw_grouped[gi % 2][:, k0:k1, :].rearrange("p k t -> p (k t)"),
+            )
+
+        def group_y(engine, gi, d0, d1):
+            interleave(engine, y_grouped[gi % 2][:, d0:d1, :], y_raw[gi][:, :, d0:d1])
+
+        def quantize_y(gi):
+            nc.vector.quantize_mx(
+                out=y_codes[gi][:].bitcast(FP8X4),
+                scales=y_plane[gi][:],
+                in_=y_grouped[gi % 2][:].rearrange("p d t -> p (d t)"),
+            )
+
+        def mean_pass(kt, gi):
+            cols = slice(P * kt, P * (kt + 1))
+            nc.tensor.matmul_mx(
+                out=mean_banks[kt][:],
+                lhsT=rw_codes[gi][:, cols].bitcast(FP8X4),
+                lhsT_scale=rw_plane[gi][:, cols],
+                rhs=y_codes[gi][:].bitcast(FP8X4),
+                rhs_scale=y_plane[gi][:],
+                start=(gi == 0),
+                stop=(gi == GROUPS - 1),
+            )
+
+        def finish_nk():
+            nc.vector.tensor_reduce(
+                out=nk[:],
+                in_=nk_bank[:, : KT * TILES].rearrange("p (k i) -> p k i", i=TILES),
+                axis=mybir.AxisListType.X,
+                op=ALU.add,
+            )
+
+        def divide(kt):
+            nc.scalar.activation(out=mean[kt][:], in_=mean_banks[kt][:], func=ACT.Copy, scale=inv_nk[:, kt : kt + 1])
+            nc.sync.dma_start(out=out_0[P * kt : P * (kt + 1), :], in_=mean[kt][:])
+
+        def round_mean(kt):
+            nc.vector.tensor_copy(out=mean_bf[kt % RING][:], in_=mean[kt][:])
+
+        def turn_mean(kt):
+            words = mean_bf[kt % RING][:].bitcast(F32)
+            for u in range(2):
+                nc.tensor.transpose(mean_banks[kt][:, P * u : P * (u + 1)], words[:, u : D // 2 : 2], ident[:])
+
+        def copy_mean(kt):
+            nc.scalar.copy(
+                out=p_grouped[:, P * kt : P * (kt + 1), :].bitcast(F32),
+                in_=mean_banks[kt][:, : 2 * P].rearrange("p (u m) -> p m u", u=2),
+            )
+
+        def quantize_p(k0, k1):
+            nc.vector.quantize_mx(
+                out=p_codes[:, k0:k1].bitcast(FP8X4),
+                scales=p_plane[:, k0:k1],
+                in_=p_grouped[:, k0:k1, :].rearrange("p k t -> p (k t)"),
+            )
+
+        def store_codes(k0, k1):
+            words = out_1[0].rearrange("p m t -> p (m t)").bitcast(I32)
+            nc.sync.dma_start(out=words[:, k0:k1], in_=p_codes[:, k0:k1].bitcast(I32))
+
+        def store_plane():
+            for q in range(4):
+                nc.scalar.dma_start(
+                    out=out_2[0, 4 * q : 4 * q + 4, :].bitcast(I32), in_=p_plane[32 * q : 32 * q + 4, :].bitcast(I32)
+                )
+
+        def load_x(gi, t0, t1):
+            nc.sync.dma_start(out=x_raw[gi][:, t0:t1, :], in_=rows_of(x, gi)[:, t0:t1, :])
+
+        def load_y(gi):
+            nc.sync.dma_start(out=y_raw[gi][:], in_=rows_of(y, gi))
+
+        def load_weight(s):
+            nc.sync.dma_start(out=(eta_codes, dp_codes)[s][:].bitcast(I32), in_=(eta_words, dp_words)[s][0].bitcast(I32))
+
+        def clear_plane(s):
+            nc.vector.memset((eta_plane, dp_plane)[s][:].bitcast(U32), 0)
+
+        def load_scales(s):
+            load_plane((eta_plane, dp_plane)[s], (eta_scales, dp_scales)[s])
+
+        def clear_c():
+            nc.vector.memset(c_row[:], 0.0)
+            nc.vector.memset(minus_ones[:], -1.0)
+
+        def load_c():
+            nc.sync.dma_start(out=c_row[0:1, :], in_=c.rearrange("(o k) -> o k", o=1))
+
+        def identity():
+            make_identity(nc, ident[:])
+
+        def load_g():
+            nc.gpsimd.dma_start(out=g_raw[:], in_=g.rearrange("(p j) -> p j", j=PACK))
+
+        def load_w():
+            nc.gpsimd.dma_start(out=w_raw[:], in_=w.rearrange("(g p t) -> p g t", g=GROUPS, t=PACK))
+
+        def halve_g():
+            nc.gpsimd.tensor_scalar(out=g_half[:], in0=g_raw[:], scalar1=-0.5, scalar2=1.0, op0=ALU.mult, op1=ALU.mult)
+
+        def clear_warm():
+            nc.vector.memset(warm[:], 0.0)
+
+        def warm_table():
+            nc.scalar.activation(out=warm[:], in_=warm[:], func=ACT.Exp)
+
+        def spread_c(h):
+            nc.tensor.matmul(
+                out=banks[6 + h][:], lhsT=minus_ones[:], rhs=c_row[:, BANK * h : BANK * (h + 1)], start=True, stop=True
+            )
+
+        def copy_c(h):
+            nc.scalar.copy(out=minus_c[:, BANK * h : BANK * (h + 1)], in_=banks[6 + h][:])
+
+        def invert_nk():
+            nc.vector.reciprocal(out=inv_nk[:], in_=nk[:])
+
+        load_x(0, 0, 1)
+        clear_plane(0)
+        clear_warm()
+        identity()
+        load_x(0, 1, 4)
+        load_weight(0)
+        turn_x(0, 0, 1)
+        copy_x(True, 0, 0, 1)
+        turn_x(0, 1, 2)
+        clear_plane(1)
+        warm_table()
+        load_g()
+        load_x(1, 0, 4)
+        clear_c()
+        copy_x(True, 0, 1, 2)
+        halve_g()
+        turn_x(0, 2, 4)
+        copy_x(True, 0, 2, 4)
+        load_c()
+        load_scales(0)
+        load_scales(1)
+        square_x(0, 0, 1)
+        turn_x(1, 0, 4)
+        square_x(0, 1, 2)
+        make_q("vector", 0, 0, 1)
+        load_weight(1)
+        spread_c(0)
+        make_q("vector", 0, 1, 2)
+        square_x(0, 2, 4)
+        quantize_xq(0, 0, 1)
+        copy_x(False, 1, 0, 2)
+        load_w()
+        load_x(2, 0, 4)
+        copy_c(0)
+        make_q("pool", 0, 2, 4)
+        spread_c(1)
+        copy_c(1)
+        copy_x(False, 1, 2, 4)
+        square_x(1, 0, 2)
+        quantize_xq(0, 1, 2)
+        make_q("pool", 1, 0, 2)
+        logits(0)
+        add_c(0, 0)
+        add_c(0, 1)
+        logits(1)
+        add_c(1, 0)
+        quantize_xq(0, 2, 4)
+        square_x(1, 2, 4)
+        load_x(3, 0, 4)
+        make_q("pool", 1, 2, 4)
+        row_max(0)
+        logits(2)
+        turn_x(2, 0, 4)
+        add_c(1, 1)
+        load_y(1)
+        add_c(2, 0)
+        logits(3)
+        exponent(0)
+        add_c(2, 1)
+        invert_sum(0)
+        row_max(1)
+        row_max(2)
+        quantize_xq(1, 0, 2)
+        make_gain(0)
+        copy_x(True, 2, 2, 4)
+        add_c(3, 0)
+        exponent(1)
+        copy_x(False, 2, 0, 2)
+        add_c(3, 1)
+        column_sums(0)
+        logits(4)
+        exponent(2)
+        row_max(3)
+        square_x(2, 0, 2)
+        turn_x(3, 0, 4)
+        square_x(2, 2, 4)
+        invert_sum(2)
+        make_gain(2)
+        quantize_xq(1, 2, 4)
+        invert_sum(1)
+        exponent(3)
+        add_c(4, 0)
+        logits(5)
+        column_sums(1)
+        weigh(2)
+        add_c(4, 1)
+        add_c(5, 0)
+        load_y(3)
+        load_y(2)
+        make_q("pool", 2, 2, 4)
+        weigh(0)
+        make_gain(1)
+        add_c(5, 1)
+        row_max(4)
+        make_q("pool", 2, 0, 2)
+        logits(7)
+        invert_sum(3)
+        load_y(0)
+        copy_x(True, 3, 2, 4)
+        row_max(5)
+        column_sums(2)
+        exponent(4)
+        logits(6)
+        column_sums(3)
+        invert_sum(4)
+        make_gain(3)
+        add_c(7, 0)
+        weigh(1)
+        quantize_xq(2, 0, 4)
+        add_c(6, 0)
+        copy_x(True, 3, 0, 2)
+        add_c(6, 1)
+        logits(8)
+        weigh(3)
+        exponent(5)
+        add_c(7, 1)
+        row_max(6)
+        invert_sum(5)
+        add_c(8, 1)
+        square_x(3, 2, 4)
+        add_c(8, 0)
+        column_sums(4)
+        group_rw("pool", 0, 0, 1024)
+        row_max(7)
+        logits(9)
+        group_y("scalar", 0, 0, 512)
+        square_x(3, 0, 2)
+        logits(10)
+        exponent(7)
+        quantize_y(0)
+        make_gain(4)
+        quantize_rw(0, 0, 1024)
+        make_gain(5)
+        exponent(6)
+        row_max(8)
+        weigh(4)
+        column_sums(5)
+        invert_sum(6)
+        group_y("scalar", 1, 0, 512)
+        mean_pass(2, 0)
+        exponent(8)
+        add_c(9, 1)
+        column_sums(6)
+        add_c(10, 1)
+        make_q("pool", 3, 2, 4)
+        weigh(5)
+        invert_sum(7)
+        add_c(9, 0)
+        make_gain(7)
+        add_c(10, 0)
+        row_max(9)
+        make_q("pool", 3, 0, 2)
+        make_gain(6)
+        logits(11)
+        weigh(7)
+        row_max(10)
+        invert_sum(8)
+        quantize_xq(3, 0, 4)
+        column_sums(7)
+        weigh(6)
+        add_c(11, 0)
+        logits(12)
+        column_sums(8)
+        add_c(11, 1)
+        exponent(9)
+        row_max(11)
+        add_c(12, 0)
+        make_gain(8)
+        invert_sum(9)
+        mean_pass(0, 0)
+        logits(13)
+        group_rw("pool", 1, 0, 1024)
+        column_sums(9)
+        add_c(12, 1)
+        exponent(10)
+        row_max(12)
+        weigh(8)
+        add_c(13, 1)
+        logits(14)
+        group_y("pool", 2, 0, 512)
+        make_gain(9)
+        exponent(11)
+        invert_sum(10)
+        add_c(13, 0)
+        invert_sum(11)
+        logits(15)
+        column_sums(10)
+        row_max(13)
+        mean_pass(1, 0)
+        make_gain(10)
+        add_c(14, 1)
+        weigh(10)
+        exponent(12)
+        quantize_rw(1, 0, 1024)
+        quantize_y(1)
+        make_gain(11)
+        weigh(9)
+        exponent(13)
+        column_sums(11)
+        invert_sum(12)
+        add_c(14, 0)
+        add_c(15, 0)
+        add_c(15, 1)
+        mean_pass(1, 1)
+        row_max(15)
+        invert_sum(13)
+        weigh(11)
+        exponent(15)
+        mean_pass(3, 0)
+        make_gain(12)
+        row_max(14)
+        group_rw("pool", 2, 0, 1024)
+        invert_sum(15)
+        exponent(14)
+        make_gain(13)
+        invert_sum(14)
+        group_y("scalar", 3, 0, 512)
+        column_sums(12)
+        mean_pass(3, 1)
+        mean_pass(2, 1)
+        column_sums(13)
+        mean_pass(6, 0)
+        mean_pass(5, 0)
+        quantize_rw(2, 0, 1024)
+        column_sums(14)
+        quantize_y(2)
+        make_gain(15)
+        make_gain(14)
+        mean_pass(0, 1)
+        weigh_grouped(3, 768, 1024)
+        weigh_grouped(3, 256, 512)
+        weigh_grouped(3, 0, 256)
+        mean_pass(6, 1)
+        column_sums(15)
+        quantize_y(3)
+        mean_pass(0, 2)
+        quantize_rw(3, 256, 512)
+        mean_pass(4, 0)
+        mean_pass(1, 2)
+        mean_pass(6, 2)
+        mean_pass(2, 2)
+        mean_pass(3, 2)
+        finish_nk()
+        quantize_rw(3, 0, 256)
+        mean_pass(0, 3)
+        weigh_grouped(3, 512, 768)
+        mean_pass(1, 3)
+        mean_pass(2, 3)
+        invert_nk()
+        quantize_rw(3, 768, 1024)
+        divide(0)
+        mean_pass(4, 1)
+        mean_pass(3, 3)
+        divide(1)
+        quantize_rw(3, 512, 768)
+        mean_pass(7, 0)
+        mean_pass(4, 2)
+        mean_pass(5, 1)
+        round_mean(1)
+        round_mean(0)
+        divide(3)
+        divide(2)
+        mean_pass(4, 3)
+        mean_pass(7, 1)
+        mean_pass(6, 3)
+        mean_pass(7, 2)
+        divide(4)
+        round_mean(2)
+        mean_pass(7, 3)
+        round_mean(3)
+        mean_pass(5, 2)
+        mean_pass(5, 3)
+        divide(6)
+        turn_mean(2)
+        divide(7)
+        divide(5)
+        turn_mean(0)
+        round_mean(6)
+        copy_mean(2)
+        turn_mean(1)
+        copy_mean(0)
+        turn_mean(3)
+        turn_mean(6)
+        round_mean(4)
+        copy_mean(1)
+        round_mean(5)
+        round_mean(7)
+        copy_mean(3)
+        turn_mean(4)
+        copy_mean(4)
+        quantize_p(256, 512)
+        turn_mean(5)
+        turn_mean(7)
+        store_codes(256, 512)
+        copy_mean(6)
+        copy_mean(5)
+        copy_mean(7)
+        quantize_p(0, 256)
+        quantize_p(512, 768)
+        quantize_p(768, 1024)
+        store_codes(0, 256)
+        store_codes(512, 768)
+        store_plane()
+        store_codes(768, 1024)

@@ -23,6 +23,7 @@ TILES = GROUPS * PACK
 BANK = 512
 KT = K // P
 RING = 4
+RUN = 4
 
 
 def tile_quadraticsoftmaxweightedaverage_kernel(
@@ -40,8 +41,8 @@ def tile_quadraticsoftmaxweightedaverage_kernel(
         banks = [ps.tile([P, BANK], F32, name="bank%d" % b) for b in range(8)]
         logit_banks = [banks[0:2], banks[2:4]]
         turn_banks = banks[4:6]
-        nk_bank = banks[6]
-        mean_banks = [banks[b] for b in (7, 4, 5, 0, 1, 2, 3, 6)]
+        nk_banks = banks[6:8]
+        mean_banks = [banks[b] for b in (4, 5, 0, 1, 2, 3, 6, 7)]
 
         ident = sbuf("ident", [P, P], F32)
         minus_ones = sbuf("minus_ones", [P, P], BF16)
@@ -65,12 +66,10 @@ def tile_quadraticsoftmaxweightedaverage_kernel(
         y_codes = [sbuf("y_codes%d" % i, [P, D], U32) for i in range(GROUPS)]
         y_plane = [sbuf("y_plane%d" % i, [P, D], U8) for i in range(GROUPS)]
         neg_logits = [sbuf("neg_logits%d" % i, [P, K], F32) for i in range(3)]
-        expo = sbuf("expo", [P, PACK, K], F32)
+        resp = [sbuf("resp%d" % i, [P, PACK, K], F32) for i in range(2)]
         neg_max = sbuf("neg_max", [P, TILES], F32)
         row_sum = sbuf("row_sum", [P, TILES], F32)
         inv_sum = sbuf("inv_sum", [P, TILES], F32)
-        gain = sbuf("gain", [P, TILES], F32)
-        rw_rows = [sbuf("rw_rows%d" % i, [P, PACK, K], BF16) for i in range(2)]
         rw_grouped = [sbuf("rw_grouped%d" % i, [P, K, PACK], BF16) for i in range(2)]
         rw_codes = [sbuf("rw_codes%d" % i, [P, K], U32) for i in range(GROUPS)]
         rw_plane = [sbuf("rw_plane%d" % i, [P, K], U8) for i in range(GROUPS)]
@@ -81,6 +80,12 @@ def tile_quadraticsoftmaxweightedaverage_kernel(
         p_grouped = sbuf("p_grouped", [P, K, PACK], BF16)
         p_codes = sbuf("p_codes", [P, K], U32)
         p_plane = sbuf("p_plane", [P, K], U8)
+
+        def move(engine, dst, src):
+            if engine == "vector":
+                nc.vector.tensor_copy(out=dst, in_=src)
+            else:
+                nc.scalar.copy(out=dst, in_=src)
 
         def rows_of(src, gi):
             return src[P * PACK * gi : P * PACK * (gi + 1), :].rearrange("(p t) d -> p t d", t=PACK)
@@ -98,13 +103,10 @@ def tile_quadraticsoftmaxweightedaverage_kernel(
                     col = (2 * (t % 2) + u) * P
                     nc.tensor.transpose(turn_banks[t // 2][:, col : col + P], words[:, u : D // 2 : 2], ident[:])
 
-        def copy_x(on_vector, gi, t0, t1):
+        def copy_x(engine, gi, t0, t1):
             src = turn_banks[t0 // 2][:].rearrange("p (t u m) -> p t m u", t=2, u=2)[:, t0 % 2 : t0 % 2 + t1 - t0]
             dst = xq[gi % 2][:, t0:t1, 0].bitcast(F32)
-            if on_vector:
-                nc.vector.tensor_copy(out=dst, in_=src)
-            else:
-                nc.scalar.copy(out=dst, in_=src)
+            move(engine, dst, src)
 
         def square_x(gi, t0, t1):
             nc.scalar.activation(out=sq[gi % 2][:, t0:t1], in_=xq[gi % 2][:, t0:t1, 0], func=ACT.Square)
@@ -124,19 +126,18 @@ def tile_quadraticsoftmaxweightedaverage_kernel(
                 in_=xq[gi % 2][:, t0:t1].rearrange("p t s m j -> p (t s m j)"),
             )
 
-        def logits(i):
+        def logits(i, h):
             gi, t = divmod(i, PACK)
-            for h in range(2):
-                for s, (codes, plane) in enumerate(((eta_codes, eta_plane), (dp_codes, dp_plane))):
-                    nc.tensor.matmul_mx(
-                        out=logit_banks[i % 2][h][:],
-                        lhsT=xq_codes[gi][:, t, s, :].bitcast(FP8X4),
-                        lhsT_scale=xq_plane[gi][:, t, s, :],
-                        rhs=codes[:, 2 * BANK * h : 2 * BANK * (h + 1)].bitcast(FP4X4),
-                        rhs_scale=plane[:, BANK * h : BANK * (h + 1)],
-                        start=(s == 0),
-                        stop=(s == 1),
-                    )
+            for s, (codes, plane) in enumerate(((eta_codes, eta_plane), (dp_codes, dp_plane))):
+                nc.tensor.matmul_mx(
+                    out=logit_banks[i % 2][h][:],
+                    lhsT=xq_codes[gi][:, t, s, :].bitcast(FP8X4),
+                    lhsT_scale=xq_plane[gi][:, t, s, :],
+                    rhs=codes[:, 2 * BANK * h : 2 * BANK * (h + 1)].bitcast(FP4X4),
+                    rhs_scale=plane[:, BANK * h : BANK * (h + 1)],
+                    start=(s == 0),
+                    stop=(s == 1),
+                )
 
         def add_c(i, h):
             cols = slice(BANK * h, BANK * (h + 1))
@@ -151,7 +152,7 @@ def tile_quadraticsoftmaxweightedaverage_kernel(
 
         def exponent(i):
             nc.scalar.activation(
-                out=expo[:, i % PACK, :],
+                out=resp[i // PACK % 2][:, i % PACK, :],
                 in_=neg_logits[i % 3][:],
                 func=ACT.Exp,
                 bias=neg_max[:, i : i + 1],
@@ -162,35 +163,35 @@ def tile_quadraticsoftmaxweightedaverage_kernel(
         def invert_sum(i):
             nc.vector.reciprocal(out=inv_sum[:, i : i + 1], in_=row_sum[:, i : i + 1])
 
-        def make_gain(i):
-            gi, t = divmod(i, PACK)
-            nc.scalar.activation(
-                out=gain[:, i : i + 1], in_=w_raw[:, gi, t : t + 1], func=ACT.Copy, scale=inv_sum[:, i : i + 1]
-            )
+        def normalise(engine, i, k0, k1):
+            row = resp[i // PACK % 2][:, i % PACK, k0:k1]
+            if engine == "scalar":
+                nc.scalar.activation(out=row, in_=row, func=ACT.Copy, scale=inv_sum[:, i : i + 1])
+            elif engine == "pool":
+                nc.gpsimd.tensor_scalar(
+                    out=row, in0=row, scalar1=inv_sum[:, i : i + 1], scalar2=1.0, op0=ALU.mult, op1=ALU.mult
+                )
+            else:
+                nc.vector.tensor_scalar(out=row, in0=row, scalar1=inv_sum[:, i : i + 1], scalar2=None, op0=ALU.mult)
 
-        def weigh(i):
-            gi, t = divmod(i, PACK)
-            nc.scalar.activation(
-                out=rw_rows[gi % 2][:, t, :], in_=expo[:, t, :], func=ACT.Copy, scale=gain[:, i : i + 1]
-            )
-
-        def weigh_grouped(gi, k0, k1):
-            nc.vector.tensor_tensor(
-                out=rw_grouped[gi % 2][:, k0:k1, :].rearrange("p (c i) t -> p c t i", i=PACK),
-                in0=expo[:, :, k0:k1].rearrange("p t (c i) -> p c t i", i=PACK),
-                in1=gain[:, PACK * gi : PACK * (gi + 1)].unsqueeze(1).unsqueeze(3).to_broadcast([P, (k1 - k0) // PACK, PACK, PACK]),
+        def weigh(engine, gi, k0, k1):
+            (nc.gpsimd if engine == "pool" else nc.vector).tensor_tensor(
+                out=rw_grouped[gi % 2][:, k0:k1, :].rearrange("p (c i) t -> p c t i", i=RUN),
+                in0=resp[gi % 2][:, :, k0:k1].rearrange("p t (c i) -> p c t i", i=RUN),
+                in1=w_raw[:, gi, :].unsqueeze(1).unsqueeze(3).to_broadcast([P, (k1 - k0) // RUN, PACK, RUN]),
                 op=ALU.mult,
             )
 
-        def column_sums(i):
-            for kt in range(KT):
-                col = kt * TILES + i
+        def column_sums(i, half):
+            for q in range(PACK):
+                kt = PACK * half + q
                 nc.tensor.matmul(
-                    out=nk_bank[:, col : col + 1],
-                    lhsT=expo[:, i % PACK, P * kt : P * (kt + 1)],
-                    rhs=inv_sum[:, i : i + 1],
-                    start=True,
-                    stop=True,
+                    out=nk_banks[half][:, P * q : P * (q + 1)],
+                    lhsT=resp[i // PACK % 2][:, i % PACK, P * kt : P * (kt + 1)],
+                    rhs=ident[:],
+                    start=(i == 0 and q == 0),
+                    stop=(i == TILES - 1 and q == PACK - 1),
+                    is_transpose=True,
                 )
 
         def interleave(engine, dst, src):
@@ -201,9 +202,6 @@ def tile_quadraticsoftmaxweightedaverage_kernel(
                 nc.scalar.copy(out=dst, in_=src)
             else:
                 nc.vector.tensor_copy(out=dst, in_=src)
-
-        def group_rw(engine, gi, k0, k1):
-            interleave(engine, rw_grouped[gi % 2][:, k0:k1, :], rw_rows[gi % 2][:, :, k0:k1])
 
         def quantize_rw(gi, k0, k1):
             nc.vector.quantize_mx(
@@ -234,30 +232,40 @@ def tile_quadraticsoftmaxweightedaverage_kernel(
                 stop=(gi == GROUPS - 1),
             )
 
-        def finish_nk():
+        def finish_nk(half):
             nc.vector.tensor_reduce(
-                out=nk[:],
-                in_=nk_bank[:, : KT * TILES].rearrange("p (k i) -> p k i", i=TILES),
+                out=nk[:, PACK * half : PACK * (half + 1)],
+                in_=nk_banks[half][:].rearrange("p (k i) -> p k i", i=P),
                 axis=mybir.AxisListType.X,
                 op=ALU.add,
             )
 
-        def divide(kt):
-            nc.scalar.activation(out=mean[kt][:], in_=mean_banks[kt][:], func=ACT.Copy, scale=inv_nk[:, kt : kt + 1])
+        def divide(engine, kt):
+            if engine == "vector":
+                nc.vector.tensor_scalar(
+                    out=mean[kt][:], in0=mean_banks[kt][:], scalar1=inv_nk[:, kt : kt + 1], scalar2=None, op0=ALU.mult
+                )
+            else:
+                nc.scalar.activation(
+                    out=mean[kt][:], in_=mean_banks[kt][:], func=ACT.Copy, scale=inv_nk[:, kt : kt + 1]
+                )
+
+        def store_mean(kt):
             nc.sync.dma_start(out=out_0[P * kt : P * (kt + 1), :], in_=mean[kt][:])
 
-        def round_mean(kt):
-            nc.vector.tensor_copy(out=mean_bf[kt % RING][:], in_=mean[kt][:])
+        def round_mean(engine, kt):
+            move(engine, mean_bf[kt % RING][:], mean[kt][:])
 
         def turn_mean(kt):
             words = mean_bf[kt % RING][:].bitcast(F32)
             for u in range(2):
                 nc.tensor.transpose(mean_banks[kt][:, P * u : P * (u + 1)], words[:, u : D // 2 : 2], ident[:])
 
-        def copy_mean(kt):
-            nc.scalar.copy(
-                out=p_grouped[:, P * kt : P * (kt + 1), :].bitcast(F32),
-                in_=mean_banks[kt][:, : 2 * P].rearrange("p (u m) -> p m u", u=2),
+        def copy_mean(engine, kt):
+            move(
+                engine,
+                p_grouped[:, P * kt : P * (kt + 1), :].bitcast(F32),
+                mean_banks[kt][:, : 2 * P].rearrange("p (u m) -> p m u", u=2),
             )
 
         def quantize_p(k0, k1):
@@ -322,313 +330,361 @@ def tile_quadraticsoftmaxweightedaverage_kernel(
                 out=banks[6 + h][:], lhsT=minus_ones[:], rhs=c_row[:, BANK * h : BANK * (h + 1)], start=True, stop=True
             )
 
-        def copy_c(h):
-            nc.scalar.copy(out=minus_c[:, BANK * h : BANK * (h + 1)], in_=banks[6 + h][:])
+        def copy_c(engine, h):
+            move(engine, minus_c[:, BANK * h : BANK * (h + 1)], banks[6 + h][:])
 
-        def invert_nk():
-            nc.vector.reciprocal(out=inv_nk[:], in_=nk[:])
+        def invert_nk(half):
+            cols = slice(PACK * half, PACK * (half + 1))
+            nc.vector.reciprocal(out=inv_nk[:, cols], in_=nk[:, cols])
 
         load_x(0, 0, 1)
-        clear_plane(0)
-        clear_warm()
         identity()
         load_x(0, 1, 4)
-        load_weight(0)
-        turn_x(0, 0, 1)
-        copy_x(True, 0, 0, 1)
-        turn_x(0, 1, 2)
-        clear_plane(1)
-        warm_table()
+        clear_plane(0)
         load_g()
-        load_x(1, 0, 4)
+        clear_plane(1)
+        turn_x(0, 0, 1)
         clear_c()
-        copy_x(True, 0, 1, 2)
-        halve_g()
-        turn_x(0, 2, 4)
-        copy_x(True, 0, 2, 4)
         load_c()
+        load_x(1, 0, 4)
         load_scales(0)
+        clear_warm()
+        warm_table()
         load_scales(1)
+        copy_x("vector", 0, 0, 1)
+        turn_x(0, 2, 4)
+        turn_x(0, 1, 2)
         square_x(0, 0, 1)
-        turn_x(1, 0, 4)
-        square_x(0, 1, 2)
-        make_q("vector", 0, 0, 1)
-        load_weight(1)
-        spread_c(0)
-        make_q("vector", 0, 1, 2)
-        square_x(0, 2, 4)
-        quantize_xq(0, 0, 1)
-        copy_x(False, 1, 0, 2)
+        copy_x("scalar", 0, 1, 2)
+        load_weight(0)
+        copy_x("vector", 0, 2, 4)
+        turn_x(1, 2, 4)
         load_w()
-        load_x(2, 0, 4)
-        copy_c(0)
-        make_q("pool", 0, 2, 4)
-        spread_c(1)
-        copy_c(1)
-        copy_x(False, 1, 2, 4)
-        square_x(1, 0, 2)
-        quantize_xq(0, 1, 2)
-        make_q("pool", 1, 0, 2)
-        logits(0)
-        add_c(0, 0)
-        add_c(0, 1)
-        logits(1)
-        add_c(1, 0)
-        quantize_xq(0, 2, 4)
-        square_x(1, 2, 4)
-        load_x(3, 0, 4)
-        make_q("pool", 1, 2, 4)
-        row_max(0)
-        logits(2)
-        turn_x(2, 0, 4)
-        add_c(1, 1)
-        load_y(1)
-        add_c(2, 0)
-        logits(3)
-        exponent(0)
-        add_c(2, 1)
-        invert_sum(0)
-        row_max(1)
-        row_max(2)
-        quantize_xq(1, 0, 2)
-        make_gain(0)
-        copy_x(True, 2, 2, 4)
-        add_c(3, 0)
-        exponent(1)
-        copy_x(False, 2, 0, 2)
-        add_c(3, 1)
-        column_sums(0)
-        logits(4)
-        exponent(2)
-        row_max(3)
-        square_x(2, 0, 2)
-        turn_x(3, 0, 4)
-        square_x(2, 2, 4)
-        invert_sum(2)
-        make_gain(2)
-        quantize_xq(1, 2, 4)
-        invert_sum(1)
-        exponent(3)
-        add_c(4, 0)
-        logits(5)
-        column_sums(1)
-        weigh(2)
-        add_c(4, 1)
-        add_c(5, 0)
-        load_y(3)
-        load_y(2)
-        make_q("pool", 2, 2, 4)
-        weigh(0)
-        make_gain(1)
-        add_c(5, 1)
-        row_max(4)
-        make_q("pool", 2, 0, 2)
-        logits(7)
-        invert_sum(3)
+        halve_g()
+        square_x(0, 1, 2)
         load_y(0)
-        copy_x(True, 3, 2, 4)
-        row_max(5)
-        column_sums(2)
-        exponent(4)
-        logits(6)
-        column_sums(3)
-        invert_sum(4)
-        make_gain(3)
-        add_c(7, 0)
-        weigh(1)
-        quantize_xq(2, 0, 4)
-        add_c(6, 0)
-        copy_x(True, 3, 0, 2)
-        add_c(6, 1)
-        logits(8)
-        weigh(3)
-        exponent(5)
-        add_c(7, 1)
-        row_max(6)
-        invert_sum(5)
-        add_c(8, 1)
-        square_x(3, 2, 4)
-        add_c(8, 0)
-        column_sums(4)
-        group_rw("pool", 0, 0, 1024)
-        row_max(7)
-        logits(9)
+        load_weight(1)
+        make_q("vector", 0, 0, 1)
+        spread_c(1)
+        square_x(0, 2, 4)
+        make_q("vector", 0, 1, 2)
+        quantize_xq(0, 0, 1)
+        quantize_xq(0, 1, 2)
+        copy_x("vector", 1, 2, 4)
+        copy_c("scalar", 1)
         group_y("scalar", 0, 0, 512)
-        square_x(3, 0, 2)
-        logits(10)
-        exponent(7)
+        spread_c(0)
+        copy_c("vector", 0)
+        turn_x(1, 0, 2)
+        logits(0, 1)
+        copy_x("vector", 1, 0, 2)
+        make_q("pool", 0, 2, 4)
+        load_y(2)
+        add_c(0, 1)
+        load_x(2, 0, 4)
+        logits(1, 1)
+        quantize_xq(0, 2, 4)
         quantize_y(0)
-        make_gain(4)
-        quantize_rw(0, 0, 1024)
-        make_gain(5)
-        exponent(6)
-        row_max(8)
-        weigh(4)
-        column_sums(5)
-        invert_sum(6)
+        load_y(3)
+        logits(1, 0)
+        logits(0, 0)
+        turn_x(2, 0, 2)
+        square_x(1, 0, 2)
+        add_c(1, 0)
+        add_c(1, 1)
+        make_q("pool", 1, 0, 2)
+        square_x(1, 2, 4)
+        add_c(0, 0)
+        row_max(1)
+        turn_x(2, 2, 4)
+        copy_x("scalar", 2, 0, 2)
+        copy_x("scalar", 2, 2, 4)
+        logits(2, 1)
+        square_x(2, 0, 2)
+        row_max(0)
+        load_x(3, 0, 4)
+        add_c(2, 1)
+        logits(2, 0)
+        turn_x(3, 2, 4)
+        add_c(2, 0)
+        turn_x(3, 0, 2)
+        logits(3, 1)
+        make_q("pool", 1, 2, 4)
+        exponent(1)
+        invert_sum(1)
+        make_q("pool", 2, 0, 2)
+        quantize_xq(1, 0, 2)
+        quantize_xq(1, 2, 4)
+        exponent(0)
+        logits(3, 0)
+        invert_sum(0)
+        square_x(2, 2, 4)
+        normalise("scalar", 0, 0, 1024)
+        add_c(3, 1)
+        normalise("scalar", 1, 0, 1024)
+        logits(4, 1)
+        logits(4, 0)
+        add_c(3, 0)
+        logits(5, 0)
+        column_sums(0, 0)
+        row_max(2)
+        row_max(3)
+        column_sums(0, 1)
+        make_q("pool", 2, 2, 4)
+        exponent(2)
+        column_sums(1, 1)
+        exponent(3)
+        column_sums(1, 0)
+        add_c(4, 1)
+        add_c(4, 0)
+        logits(5, 1)
+        invert_sum(2)
+        load_y(1)
+        normalise("scalar", 2, 0, 1024)
+        add_c(5, 0)
+        quantize_xq(2, 0, 2)
+        invert_sum(3)
+        quantize_xq(2, 2, 4)
+        logits(6, 0)
+        logits(6, 1)
+        add_c(6, 0)
+        row_max(4)
+        copy_x("scalar", 3, 0, 2)
+        column_sums(2, 1)
+        logits(7, 0)
+        normalise("pool", 3, 0, 1024)
         group_y("scalar", 1, 0, 512)
-        mean_pass(2, 0)
-        exponent(8)
+        exponent(4)
+        add_c(6, 1)
+        add_c(5, 1)
+        row_max(5)
+        column_sums(2, 0)
+        column_sums(3, 0)
+        copy_x("scalar", 3, 2, 4)
+        exponent(5)
+        logits(8, 0)
+        weigh("pool", 0, 512, 768)
+        logits(7, 1)
+        add_c(7, 1)
+        invert_sum(4)
+        column_sums(3, 1)
+        logits(9, 1)
+        normalise("scalar", 4, 0, 1024)
+        add_c(7, 0)
+        row_max(6)
+        exponent(6)
+        invert_sum(5)
+        logits(8, 1)
+        add_c(8, 0)
+        weigh("vector", 0, 768, 1024)
+        add_c(8, 1)
+        column_sums(4, 1)
+        row_max(7)
+        column_sums(4, 0)
+        logits(9, 0)
+        row_max(8)
+        logits(10, 0)
+        invert_sum(6)
+        normalise("scalar", 5, 0, 1024)
+        weigh("pool", 0, 256, 512)
+        weigh("pool", 0, 0, 256)
+        column_sums(5, 1)
+        square_x(3, 0, 2)
+        column_sums(5, 0)
+        exponent(7)
         add_c(9, 1)
-        column_sums(6)
+        logits(10, 1)
+        logits(11, 1)
         add_c(10, 1)
-        make_q("pool", 3, 2, 4)
-        weigh(5)
-        invert_sum(7)
-        add_c(9, 0)
-        make_gain(7)
-        add_c(10, 0)
-        row_max(9)
+        exponent(8)
         make_q("pool", 3, 0, 2)
-        make_gain(6)
-        logits(11)
-        weigh(7)
-        row_max(10)
-        invert_sum(8)
-        quantize_xq(3, 0, 4)
-        column_sums(7)
-        weigh(6)
-        add_c(11, 0)
-        logits(12)
-        column_sums(8)
+        invert_sum(7)
+        normalise("scalar", 6, 0, 1024)
+        add_c(9, 0)
+        square_x(3, 2, 4)
         add_c(11, 1)
-        exponent(9)
-        row_max(11)
-        add_c(12, 0)
-        make_gain(8)
-        invert_sum(9)
+        quantize_rw(0, 0, 512)
+        quantize_y(1)
+        logits(11, 0)
+        column_sums(6, 0)
         mean_pass(0, 0)
-        logits(13)
-        group_rw("pool", 1, 0, 1024)
-        column_sums(9)
-        add_c(12, 1)
+        column_sums(6, 1)
+        normalise("scalar", 7, 0, 1024)
+        quantize_xq(3, 0, 2)
+        logits(12, 1)
+        logits(13, 1)
+        row_max(9)
+        make_q("pool", 3, 2, 4)
+        invert_sum(8)
+        add_c(10, 0)
+        add_c(11, 0)
+        weigh("pool", 1, 0, 256)
+        column_sums(7, 0)
+        group_y("scalar", 3, 0, 512)
+        row_max(10)
+        exponent(9)
+        column_sums(7, 1)
+        row_max(11)
+        normalise("scalar", 8, 0, 1024)
+        logits(12, 0)
+        add_c(12, 0)
+        logits(13, 0)
+        column_sums(8, 0)
+        invert_sum(9)
+        weigh("vector", 1, 256, 512)
+        quantize_xq(3, 2, 4)
         exponent(10)
-        row_max(12)
-        weigh(8)
-        add_c(13, 1)
-        logits(14)
-        group_y("pool", 2, 0, 512)
-        make_gain(9)
         exponent(11)
         invert_sum(10)
+        normalise("scalar", 9, 0, 1024)
+        add_c(13, 1)
+        normalise("scalar", 10, 0, 1024)
+        column_sums(8, 1)
+        weigh("pool", 1, 512, 768)
+        logits(14, 0)
+        weigh("pool", 1, 768, 1024)
+        logits(15, 1)
+        add_c(12, 1)
+        column_sums(9, 0)
         add_c(13, 0)
-        invert_sum(11)
-        logits(15)
-        column_sums(10)
+        column_sums(9, 1)
+        group_y("scalar", 2, 0, 512)
+        logits(14, 1)
+        row_max(12)
         row_max(13)
-        mean_pass(1, 0)
-        make_gain(10)
-        add_c(14, 1)
-        weigh(10)
-        exponent(12)
-        quantize_rw(1, 0, 1024)
-        quantize_y(1)
-        make_gain(11)
-        weigh(9)
-        exponent(13)
-        column_sums(11)
-        invert_sum(12)
         add_c(14, 0)
+        invert_sum(11)
+        column_sums(10, 0)
+        column_sums(10, 1)
+        normalise("pool", 11, 0, 1024)
+        add_c(14, 1)
+        row_max(14)
+        quantize_rw(1, 0, 512)
+        exponent(13)
+        quantize_rw(1, 512, 1024)
+        quantize_y(3)
+        exponent(12)
+        logits(15, 0)
+        column_sums(11, 1)
+        invert_sum(12)
         add_c(15, 0)
         add_c(15, 1)
-        mean_pass(1, 1)
-        row_max(15)
-        invert_sum(13)
-        weigh(11)
-        exponent(15)
-        mean_pass(3, 0)
-        make_gain(12)
-        row_max(14)
-        group_rw("pool", 2, 0, 1024)
-        invert_sum(15)
         exponent(14)
-        make_gain(13)
+        column_sums(11, 0)
+        weigh("pool", 2, 0, 256)
+        mean_pass(1, 0)
+        normalise("scalar", 12, 0, 1024)
+        mean_pass(2, 0)
+        invert_sum(13)
+        mean_pass(1, 1)
         invert_sum(14)
-        group_y("scalar", 3, 0, 512)
-        column_sums(12)
-        mean_pass(3, 1)
-        mean_pass(2, 1)
-        column_sums(13)
-        mean_pass(6, 0)
-        mean_pass(5, 0)
-        quantize_rw(2, 0, 1024)
-        column_sums(14)
+        row_max(15)
+        mean_pass(3, 0)
+        column_sums(12, 1)
+        quantize_rw(0, 512, 1024)
+        weigh("vector", 2, 256, 512)
+        column_sums(12, 0)
+        normalise("scalar", 13, 0, 1024)
+        exponent(15)
+        invert_sum(15)
         quantize_y(2)
-        make_gain(15)
-        make_gain(14)
+        normalise("scalar", 14, 0, 1024)
+        mean_pass(2, 1)
+        normalise("scalar", 15, 0, 1024)
+        column_sums(13, 1)
+        mean_pass(5, 0)
+        column_sums(13, 0)
+        weigh("vector", 2, 768, 1024)
+        quantize_rw(2, 0, 512)
+        mean_pass(3, 1)
         mean_pass(0, 1)
-        weigh_grouped(3, 768, 1024)
-        weigh_grouped(3, 256, 512)
-        weigh_grouped(3, 0, 256)
-        mean_pass(6, 1)
-        column_sums(15)
-        quantize_y(3)
-        mean_pass(0, 2)
-        quantize_rw(3, 256, 512)
         mean_pass(4, 0)
+        column_sums(14, 1)
+        column_sums(14, 0)
+        column_sums(15, 0)
+        weigh("vector", 3, 0, 256)
+        finish_nk(0)
         mean_pass(1, 2)
-        mean_pass(6, 2)
-        mean_pass(2, 2)
-        mean_pass(3, 2)
-        finish_nk()
         quantize_rw(3, 0, 256)
-        mean_pass(0, 3)
-        weigh_grouped(3, 512, 768)
-        mean_pass(1, 3)
-        mean_pass(2, 3)
-        invert_nk()
-        quantize_rw(3, 768, 1024)
-        divide(0)
+        invert_nk(0)
+        mean_pass(3, 2)
         mean_pass(4, 1)
-        mean_pass(3, 3)
-        divide(1)
-        quantize_rw(3, 512, 768)
-        mean_pass(7, 0)
-        mean_pass(4, 2)
+        mean_pass(0, 2)
+        mean_pass(1, 3)
+        mean_pass(0, 3)
+        weigh("vector", 3, 256, 512)
+        mean_pass(6, 0)
+        weigh("vector", 2, 512, 768)
+        column_sums(15, 1)
+        quantize_rw(3, 256, 512)
         mean_pass(5, 1)
-        round_mean(1)
-        round_mean(0)
-        divide(3)
-        divide(2)
-        mean_pass(4, 3)
-        mean_pass(7, 1)
-        mean_pass(6, 3)
-        mean_pass(7, 2)
-        divide(4)
-        round_mean(2)
-        mean_pass(7, 3)
-        round_mean(3)
-        mean_pass(5, 2)
-        mean_pass(5, 3)
-        divide(6)
-        turn_mean(2)
-        divide(7)
-        divide(5)
-        turn_mean(0)
-        round_mean(6)
-        copy_mean(2)
+        quantize_rw(2, 512, 1024)
+        mean_pass(6, 1)
+        mean_pass(2, 2)
+        weigh("vector", 3, 512, 768)
+        divide("scalar", 1)
+        divide("scalar", 0)
+        round_mean("scalar", 1)
+        finish_nk(1)
+        mean_pass(2, 3)
         turn_mean(1)
-        copy_mean(0)
-        turn_mean(3)
-        turn_mean(6)
-        round_mean(4)
-        copy_mean(1)
-        round_mean(5)
-        round_mean(7)
-        copy_mean(3)
-        turn_mean(4)
-        copy_mean(4)
-        quantize_p(256, 512)
-        turn_mean(5)
-        turn_mean(7)
-        store_codes(256, 512)
-        copy_mean(6)
-        copy_mean(5)
-        copy_mean(7)
+        mean_pass(3, 3)
+        store_mean(0)
+        round_mean("scalar", 0)
+        divide("scalar", 2)
+        copy_mean("scalar", 1)
+        round_mean("scalar", 2)
+        turn_mean(0)
+        mean_pass(4, 2)
+        mean_pass(5, 2)
+        quantize_rw(3, 512, 768)
+        mean_pass(6, 2)
+        weigh("vector", 3, 768, 1024)
+        mean_pass(4, 3)
+        store_mean(1)
+        copy_mean("scalar", 0)
+        store_mean(2)
+        divide("scalar", 3)
+        mean_pass(7, 0)
+        invert_nk(1)
+        mean_pass(5, 3)
+        quantize_rw(3, 768, 1024)
+        mean_pass(7, 1)
+        divide("vector", 4)
+        mean_pass(7, 2)
+        round_mean("scalar", 3)
         quantize_p(0, 256)
-        quantize_p(512, 768)
-        quantize_p(768, 1024)
+        mean_pass(7, 3)
+        mean_pass(6, 3)
+        divide("vector", 7)
+        turn_mean(3)
+        round_mean("vector", 4)
+        round_mean("vector", 7)
+        divide("scalar", 5)
+        turn_mean(2)
+        store_mean(3)
+        round_mean("scalar", 5)
+        turn_mean(5)
+        store_mean(4)
+        store_mean(5)
+        turn_mean(4)
+        divide("scalar", 6)
+        round_mean("vector", 6)
+        copy_mean("scalar", 2)
+        turn_mean(7)
+        copy_mean("scalar", 5)
         store_codes(0, 256)
+        store_mean(7)
+        copy_mean("vector", 3)
+        copy_mean("scalar", 4)
+        copy_mean("vector", 7)
+        quantize_p(256, 512)
+        quantize_p(512, 768)
+        store_mean(6)
+        store_codes(256, 512)
         store_codes(512, 768)
+        turn_mean(6)
+        copy_mean("scalar", 6)
+        quantize_p(768, 1024)
         store_plane()
         store_codes(768, 1024)

@@ -23,7 +23,8 @@ TILES = GROUPS * PACK
 BANK = 512
 KT = K // P
 RING = 4
-RUN = 4
+RUN = 2
+EARLY = 2 * PACK
 
 
 def tile_quadraticsoftmaxweightedaverage_kernel(
@@ -56,12 +57,16 @@ def tile_quadraticsoftmaxweightedaverage_kernel(
         dp_codes = sbuf("dp_codes", [P, 2 * K], U8)
         eta_plane = sbuf("eta_plane", [P, K], U8)
         dp_plane = sbuf("dp_plane", [P, K], U8)
-        x_raw = [sbuf("x_raw%d" % i, [P, PACK, D], BF16) for i in range(GROUPS)]
-        y_raw = [sbuf("y_raw%d" % i, [P, PACK, D], BF16) for i in range(GROUPS)]
-        xq = [sbuf("xq%d" % i, [P, PACK, 2, P, PACK], BF16) for i in range(2)]
+        x_raw = [sbuf("x_raw%d" % i, [P, PACK, D], BF16) for i in range(2)]
+        y_raw = [sbuf("y_raw%d" % i, [P, PACK, D], BF16) for i in range(2)]
+        x_grouped = [sbuf("x_grouped%d" % i, [P, PACK, P, PACK], BF16) for i in range(2)]
+        q_grouped = [sbuf("q_grouped%d" % i, [P, PACK, P, PACK], BF16) for i in range(2)]
+        stage = sbuf("stage", [P, 4 * P, PACK], BF16)
         sq = [sbuf("sq%d" % i, [P, PACK, P, PACK], F32) for i in range(2)]
-        xq_codes = [sbuf("xq_codes%d" % i, [P, PACK, 2, P], U32) for i in range(GROUPS)]
-        xq_plane = [sbuf("xq_plane%d" % i, [P, PACK, 2, P], U8) for i in range(GROUPS)]
+        x_codes = sbuf("x_codes", [P, N], U32)
+        x_plane = sbuf("x_plane", [P, N], U8)
+        q_codes = sbuf("q_codes", [P, N], U32)
+        q_plane = sbuf("q_plane", [P, N], U8)
         y_grouped = [sbuf("y_grouped%d" % i, [P, D, PACK], BF16) for i in range(2)]
         y_codes = [sbuf("y_codes%d" % i, [P, D], U32) for i in range(GROUPS)]
         y_plane = [sbuf("y_plane%d" % i, [P, D], U8) for i in range(GROUPS)]
@@ -73,6 +78,9 @@ def tile_quadraticsoftmaxweightedaverage_kernel(
         rw_grouped = [sbuf("rw_grouped%d" % i, [P, K, PACK], BF16) for i in range(2)]
         rw_codes = [sbuf("rw_codes%d" % i, [P, K], U32) for i in range(GROUPS)]
         rw_plane = [sbuf("rw_plane%d" % i, [P, K], U8) for i in range(GROUPS)]
+        gain = sbuf("gain", [P, TILES], F32)
+        rw_rows = [sbuf("rw_rows%d" % i, [P, PACK, K], BF16) for i in range(2)]
+        early_nk = sbuf("early_nk", [P, K], F32)
         nk = sbuf("nk", [P, KT], F32)
         inv_nk = sbuf("inv_nk", [P, KT], F32)
         mean = [sbuf("mean%d" % i, [P, D], F32) for i in range(KT)]
@@ -98,41 +106,52 @@ def tile_quadraticsoftmaxweightedaverage_kernel(
 
         def turn_x(gi, t0, t1):
             for t in range(t0, t1):
-                words = x_raw[gi][:, t, :].bitcast(F32)
+                words = x_raw[gi % 2][:, t, :].bitcast(F32)
                 for u in range(2):
                     col = (2 * (t % 2) + u) * P
                     nc.tensor.transpose(turn_banks[t // 2][:, col : col + P], words[:, u : D // 2 : 2], ident[:])
 
         def copy_x(engine, gi, t0, t1):
             src = turn_banks[t0 // 2][:].rearrange("p (t u m) -> p t m u", t=2, u=2)[:, t0 % 2 : t0 % 2 + t1 - t0]
-            dst = xq[gi % 2][:, t0:t1, 0].bitcast(F32)
+            dst = x_grouped[gi % 2][:, t0:t1].bitcast(F32)
             move(engine, dst, src)
 
         def square_x(gi, t0, t1):
-            nc.scalar.activation(out=sq[gi % 2][:, t0:t1], in_=xq[gi % 2][:, t0:t1, 0], func=ACT.Square)
+            nc.scalar.activation(out=sq[gi % 2][:, t0:t1], in_=x_grouped[gi % 2][:, t0:t1], func=ACT.Square)
+
+        def staged(engine, own):
+            return stage[:, : own.shape[1], :] if engine == "pool" else own
+
+        def quantize(codes, plane, grouped):
+            nc.vector.quantize_mx(out=codes.bitcast(FP8X4), scales=plane, in_=grouped.rearrange("p n j -> p (n j)"))
+
+        def q_rows(engine, gi, t0, t1):
+            return staged(engine, q_grouped[gi % 2][:, t0:t1].rearrange("p t m j -> p (t m) j"))
 
         def make_q(engine, gi, t0, t1):
             (nc.gpsimd if engine == "pool" else nc.vector).tensor_tensor(
-                out=xq[gi % 2][:, t0:t1, 1],
-                in0=sq[gi % 2][:, t0:t1],
-                in1=g_half[:].unsqueeze(1).unsqueeze(1).to_broadcast([P, t1 - t0, P, PACK]),
+                out=q_rows(engine, gi, t0, t1),
+                in0=sq[gi % 2][:, t0:t1].rearrange("p t m j -> p (t m) j"),
+                in1=g_half[:].unsqueeze(1).to_broadcast([P, (t1 - t0) * P, PACK]),
                 op=ALU.mult,
             )
 
-        def quantize_xq(gi, t0, t1):
-            nc.vector.quantize_mx(
-                out=xq_codes[gi][:, t0:t1].rearrange("p t s m -> p (t s m)").bitcast(FP8X4),
-                scales=xq_plane[gi][:, t0:t1].rearrange("p t s m -> p (t s m)"),
-                in_=xq[gi % 2][:, t0:t1].rearrange("p t s m j -> p (t s m j)"),
-            )
+        def quantize_x(gi, t0, t1):
+            cols = slice(P * (PACK * gi + t0), P * (PACK * gi + t1))
+            quantize(x_codes[:, cols], x_plane[:, cols], x_grouped[gi % 2][:, t0:t1].rearrange("p t m j -> p (t m) j"))
+
+        def quantize_q(engine, gi, t0, t1):
+            cols = slice(P * (PACK * gi + t0), P * (PACK * gi + t1))
+            quantize(q_codes[:, cols], q_plane[:, cols], q_rows(engine, gi, t0, t1))
 
         def logits(i, h):
-            gi, t = divmod(i, PACK)
-            for s, (codes, plane) in enumerate(((eta_codes, eta_plane), (dp_codes, dp_plane))):
+            cols = slice(P * i, P * (i + 1))
+            products = ((x_codes, x_plane, eta_codes, eta_plane), (q_codes, q_plane, dp_codes, dp_plane))
+            for s, (act_codes, act_plane, codes, plane) in enumerate(products):
                 nc.tensor.matmul_mx(
                     out=logit_banks[i % 2][h][:],
-                    lhsT=xq_codes[gi][:, t, s, :].bitcast(FP8X4),
-                    lhsT_scale=xq_plane[gi][:, t, s, :],
+                    lhsT=act_codes[:, cols].bitcast(FP8X4),
+                    lhsT_scale=act_plane[:, cols],
                     rhs=codes[:, 2 * BANK * h : 2 * BANK * (h + 1)].bitcast(FP4X4),
                     rhs_scale=plane[:, BANK * h : BANK * (h + 1)],
                     start=(s == 0),
@@ -175,21 +194,54 @@ def tile_quadraticsoftmaxweightedaverage_kernel(
                 nc.vector.tensor_scalar(out=row, in0=row, scalar1=inv_sum[:, i : i + 1], scalar2=None, op0=ALU.mult)
 
         def weigh(engine, gi, k0, k1):
+            run = 1 if engine == "pool" else RUN
             (nc.gpsimd if engine == "pool" else nc.vector).tensor_tensor(
-                out=rw_grouped[gi % 2][:, k0:k1, :].rearrange("p (c i) t -> p c t i", i=RUN),
-                in0=resp[gi % 2][:, :, k0:k1].rearrange("p t (c i) -> p c t i", i=RUN),
-                in1=w_raw[:, gi, :].unsqueeze(1).unsqueeze(3).to_broadcast([P, (k1 - k0) // RUN, PACK, RUN]),
+                out=staged(engine, rw_grouped[gi % 2][:, k0:k1, :]).rearrange("p (c i) t -> p c t i", i=run),
+                in0=resp[gi % 2][:, :, k0:k1].rearrange("p t (c i) -> p c t i", i=run),
+                in1=w_raw[:, gi, :].unsqueeze(1).unsqueeze(3).to_broadcast([P, (k1 - k0) // run, PACK, run]),
                 op=ALU.mult,
             )
 
+        def make_gain(i):
+            gi, t = divmod(i, PACK)
+            nc.scalar.activation(
+                out=gain[:, i : i + 1], in_=w_raw[:, gi, t : t + 1], func=ACT.Copy, scale=inv_sum[:, i : i + 1]
+            )
+
+        def weigh_row(i):
+            gi, t = divmod(i, PACK)
+            nc.scalar.activation(
+                out=rw_rows[gi % 2][:, t, :], in_=resp[gi % 2][:, t, :], func=ACT.Copy, scale=gain[:, i : i + 1]
+            )
+
+        def group_rw(engine, gi, k0, k1):
+            interleave(engine, staged(engine, rw_grouped[gi % 2][:, k0:k1, :]), rw_rows[gi % 2][:, :, k0:k1])
+
+        def early_sums(i, half):
+            nc.tensor.matmul(
+                out=nk_banks[half][:],
+                lhsT=inv_sum[:, i : i + 1].to_broadcast([P, P]),
+                rhs=resp[i // PACK % 2][:, i % PACK, BANK * half : BANK * (half + 1)],
+                start=(i == 0),
+                stop=(i == EARLY - 1),
+            )
+
+        def copy_early(engine, half):
+            dst = early_nk[:, BANK * half : BANK * (half + 1)]
+            if engine == "vector":
+                nc.vector.tensor_scalar(out=dst, in0=nk_banks[half][:], scalar1=1.0 / P, scalar2=None, op0=ALU.mult)
+            else:
+                nc.scalar.activation(out=dst, in_=nk_banks[half][:], func=ACT.Copy, scale=1.0 / P)
+
         def column_sums(i, half):
+            src = early_nk[:] if i == EARLY - 1 else resp[i // PACK % 2][:, i % PACK, :]
             for q in range(PACK):
                 kt = PACK * half + q
                 nc.tensor.matmul(
                     out=nk_banks[half][:, P * q : P * (q + 1)],
-                    lhsT=resp[i // PACK % 2][:, i % PACK, P * kt : P * (kt + 1)],
+                    lhsT=src[:, P * kt : P * (kt + 1)],
                     rhs=ident[:],
-                    start=(i == 0 and q == 0),
+                    start=(i == EARLY - 1 and q == 0),
                     stop=(i == TILES - 1 and q == PACK - 1),
                     is_transpose=True,
                 )
@@ -203,22 +255,14 @@ def tile_quadraticsoftmaxweightedaverage_kernel(
             else:
                 nc.vector.tensor_copy(out=dst, in_=src)
 
-        def quantize_rw(gi, k0, k1):
-            nc.vector.quantize_mx(
-                out=rw_codes[gi][:, k0:k1].bitcast(FP8X4),
-                scales=rw_plane[gi][:, k0:k1],
-                in_=rw_grouped[gi % 2][:, k0:k1, :].rearrange("p k t -> p (k t)"),
-            )
+        def quantize_rw(engine, gi, k0, k1):
+            quantize(rw_codes[gi][:, k0:k1], rw_plane[gi][:, k0:k1], staged(engine, rw_grouped[gi % 2][:, k0:k1, :]))
 
         def group_y(engine, gi, d0, d1):
-            interleave(engine, y_grouped[gi % 2][:, d0:d1, :], y_raw[gi][:, :, d0:d1])
+            interleave(engine, staged(engine, y_grouped[gi % 2][:, d0:d1, :]), y_raw[gi % 2][:, :, d0:d1])
 
-        def quantize_y(gi):
-            nc.vector.quantize_mx(
-                out=y_codes[gi][:].bitcast(FP8X4),
-                scales=y_plane[gi][:],
-                in_=y_grouped[gi % 2][:].rearrange("p d t -> p (d t)"),
-            )
+        def quantize_y(engine, gi, d0, d1):
+            quantize(y_codes[gi][:, d0:d1], y_plane[gi][:, d0:d1], staged(engine, y_grouped[gi % 2][:, d0:d1, :]))
 
         def mean_pass(kt, gi):
             cols = slice(P * kt, P * (kt + 1))
@@ -269,11 +313,7 @@ def tile_quadraticsoftmaxweightedaverage_kernel(
             )
 
         def quantize_p(k0, k1):
-            nc.vector.quantize_mx(
-                out=p_codes[:, k0:k1].bitcast(FP8X4),
-                scales=p_plane[:, k0:k1],
-                in_=p_grouped[:, k0:k1, :].rearrange("p k t -> p (k t)"),
-            )
+            quantize(p_codes[:, k0:k1], p_plane[:, k0:k1], p_grouped[:, k0:k1, :])
 
         def store_codes(k0, k1):
             words = out_1[0].rearrange("p m t -> p (m t)").bitcast(I32)
@@ -286,10 +326,10 @@ def tile_quadraticsoftmaxweightedaverage_kernel(
                 )
 
         def load_x(gi, t0, t1):
-            nc.sync.dma_start(out=x_raw[gi][:, t0:t1, :], in_=rows_of(x, gi)[:, t0:t1, :])
+            nc.sync.dma_start(out=x_raw[gi % 2][:, t0:t1, :], in_=rows_of(x, gi)[:, t0:t1, :])
 
         def load_y(gi):
-            nc.sync.dma_start(out=y_raw[gi][:], in_=rows_of(y, gi))
+            nc.sync.dma_start(out=y_raw[gi % 2][:], in_=rows_of(y, gi))
 
         def load_weight(s):
             nc.sync.dma_start(out=(eta_codes, dp_codes)[s][:].bitcast(I32), in_=(eta_words, dp_words)[s][0].bitcast(I32))
@@ -314,7 +354,7 @@ def tile_quadraticsoftmaxweightedaverage_kernel(
             nc.gpsimd.dma_start(out=g_raw[:], in_=g.rearrange("(p j) -> p j", j=PACK))
 
         def load_w():
-            nc.gpsimd.dma_start(out=w_raw[:], in_=w.rearrange("(g p t) -> p g t", g=GROUPS, t=PACK))
+            nc.sync.dma_start(out=w_raw[:], in_=w.rearrange("(g p t) -> p g t", g=GROUPS, t=PACK))
 
         def halve_g():
             nc.gpsimd.tensor_scalar(out=g_half[:], in0=g_raw[:], scalar1=-0.5, scalar2=1.0, op0=ALU.mult, op1=ALU.mult)
@@ -339,352 +379,387 @@ def tile_quadraticsoftmaxweightedaverage_kernel(
 
         load_x(0, 0, 1)
         identity()
+        load_w()
         load_x(0, 1, 4)
+        load_weight(1)
         clear_plane(0)
         load_g()
         clear_plane(1)
-        turn_x(0, 0, 1)
-        clear_c()
-        load_c()
-        load_x(1, 0, 4)
         load_scales(0)
+        clear_c()
         clear_warm()
         warm_table()
-        load_scales(1)
-        copy_x("vector", 0, 0, 1)
-        turn_x(0, 2, 4)
-        turn_x(0, 1, 2)
-        square_x(0, 0, 1)
-        copy_x("scalar", 0, 1, 2)
+        load_c()
+        turn_x(0, 0, 1)
+        load_x(1, 0, 4)
         load_weight(0)
-        copy_x("vector", 0, 2, 4)
-        turn_x(1, 2, 4)
-        load_w()
-        halve_g()
-        square_x(0, 1, 2)
+        copy_x("vector", 0, 0, 1)
+        turn_x(0, 1, 2)
         load_y(0)
-        load_weight(1)
+        square_x(0, 0, 1)
+        halve_g()
+        quantize_x(0, 0, 1)
+        turn_x(0, 2, 4)
+        load_scales(1)
+        copy_x("vector", 0, 1, 2)
         make_q("vector", 0, 0, 1)
+        square_x(0, 1, 2)
+        spread_c(0)
+        load_x(2, 0, 4)
+        load_y(1)
+        quantize_q("vector", 0, 0, 1)
+        copy_x("scalar", 0, 2, 4)
+        quantize_x(0, 1, 2)
+        make_q("vector", 0, 1, 2)
         spread_c(1)
         square_x(0, 2, 4)
-        make_q("vector", 0, 1, 2)
-        quantize_xq(0, 0, 1)
-        quantize_xq(0, 1, 2)
-        copy_x("vector", 1, 2, 4)
-        copy_c("scalar", 1)
-        group_y("scalar", 0, 0, 512)
-        spread_c(0)
-        copy_c("vector", 0)
         turn_x(1, 0, 2)
-        logits(0, 1)
-        copy_x("vector", 1, 0, 2)
-        make_q("pool", 0, 2, 4)
-        load_y(2)
-        add_c(0, 1)
-        load_x(2, 0, 4)
-        logits(1, 1)
-        quantize_xq(0, 2, 4)
-        quantize_y(0)
-        load_y(3)
+        copy_c("vector", 0)
+        quantize_q("vector", 0, 1, 2)
         logits(1, 0)
+        quantize_x(0, 2, 4)
+        copy_c("vector", 1)
+        group_y("scalar", 0, 0, 256)
+        make_q("pool", 0, 2, 4)
         logits(0, 0)
-        turn_x(2, 0, 2)
-        square_x(1, 0, 2)
+        copy_x("vector", 1, 0, 2)
+        logits(0, 1)
         add_c(1, 0)
-        add_c(1, 1)
-        make_q("pool", 1, 0, 2)
-        square_x(1, 2, 4)
+        group_y("scalar", 0, 256, 512)
+        turn_x(1, 2, 4)
         add_c(0, 0)
-        row_max(1)
-        turn_x(2, 2, 4)
-        copy_x("scalar", 2, 0, 2)
-        copy_x("scalar", 2, 2, 4)
-        logits(2, 1)
-        square_x(2, 0, 2)
-        row_max(0)
+        turn_x(2, 0, 2)
+        add_c(0, 1)
         load_x(3, 0, 4)
-        add_c(2, 1)
+        square_x(1, 0, 2)
+        logits(1, 1)
+        load_y(2)
+        quantize_y("scalar", 0, 0, 256)
+        quantize_x(1, 0, 2)
+        quantize_q("pool", 0, 2, 4)
+        logits(2, 1)
+        copy_x("scalar", 1, 2, 4)
+        row_max(0)
+        make_q("pool", 1, 0, 2)
+        copy_x("scalar", 2, 0, 2)
         logits(2, 0)
-        turn_x(3, 2, 4)
-        add_c(2, 0)
-        turn_x(3, 0, 2)
-        logits(3, 1)
-        make_q("pool", 1, 2, 4)
-        exponent(1)
-        invert_sum(1)
-        make_q("pool", 2, 0, 2)
-        quantize_xq(1, 0, 2)
-        quantize_xq(1, 2, 4)
-        exponent(0)
+        square_x(1, 2, 4)
+        add_c(2, 1)
         logits(3, 0)
-        invert_sum(0)
-        square_x(2, 2, 4)
-        normalise("scalar", 0, 0, 1024)
-        add_c(3, 1)
-        normalise("scalar", 1, 0, 1024)
-        logits(4, 1)
+        add_c(2, 0)
+        turn_x(2, 2, 4)
+        exponent(0)
+        add_c(1, 1)
+        turn_x(3, 0, 2)
+        quantize_x(1, 2, 4)
+        logits(3, 1)
+        quantize_q("pool", 1, 0, 2)
+        copy_x("scalar", 2, 2, 4)
+        row_max(1)
+        make_q("pool", 1, 2, 4)
         logits(4, 0)
+        square_x(2, 0, 2)
+        logits(4, 1)
+        invert_sum(0)
         add_c(3, 0)
-        logits(5, 0)
-        column_sums(0, 0)
+        turn_x(3, 2, 4)
+        exponent(1)
         row_max(2)
-        row_max(3)
-        column_sums(0, 1)
-        make_q("pool", 2, 2, 4)
-        exponent(2)
-        column_sums(1, 1)
-        exponent(3)
-        column_sums(1, 0)
-        add_c(4, 1)
+        early_sums(0, 1)
+        make_gain(0)
+        quantize_x(2, 0, 2)
+        copy_x("scalar", 3, 0, 2)
+        quantize_q("pool", 1, 2, 4)
+        early_sums(0, 0)
+        square_x(2, 2, 4)
+        add_c(3, 1)
+        make_q("pool", 2, 0, 2)
+        invert_sum(1)
         add_c(4, 0)
         logits(5, 1)
-        invert_sum(2)
-        load_y(1)
-        normalise("scalar", 2, 0, 1024)
-        add_c(5, 0)
-        quantize_xq(2, 0, 2)
-        invert_sum(3)
-        quantize_xq(2, 2, 4)
+        exponent(2)
+        row_max(3)
+        logits(5, 0)
         logits(6, 0)
-        logits(6, 1)
-        add_c(6, 0)
-        row_max(4)
-        copy_x("scalar", 3, 0, 2)
-        column_sums(2, 1)
-        logits(7, 0)
-        normalise("pool", 3, 0, 1024)
-        group_y("scalar", 1, 0, 512)
-        exponent(4)
-        add_c(6, 1)
-        add_c(5, 1)
-        row_max(5)
-        column_sums(2, 0)
-        column_sums(3, 0)
-        copy_x("scalar", 3, 2, 4)
-        exponent(5)
-        logits(8, 0)
-        weigh("pool", 0, 512, 768)
-        logits(7, 1)
-        add_c(7, 1)
-        invert_sum(4)
-        column_sums(3, 1)
-        logits(9, 1)
-        normalise("scalar", 4, 0, 1024)
-        add_c(7, 0)
-        row_max(6)
-        exponent(6)
-        invert_sum(5)
-        logits(8, 1)
-        add_c(8, 0)
-        weigh("vector", 0, 768, 1024)
-        add_c(8, 1)
-        column_sums(4, 1)
-        row_max(7)
-        column_sums(4, 0)
-        logits(9, 0)
-        row_max(8)
-        logits(10, 0)
-        invert_sum(6)
-        normalise("scalar", 5, 0, 1024)
-        weigh("pool", 0, 256, 512)
-        weigh("pool", 0, 0, 256)
-        column_sums(5, 1)
+        make_gain(1)
         square_x(3, 0, 2)
-        column_sums(5, 0)
-        exponent(7)
-        add_c(9, 1)
-        logits(10, 1)
-        logits(11, 1)
-        add_c(10, 1)
-        exponent(8)
-        make_q("pool", 3, 0, 2)
-        invert_sum(7)
-        normalise("scalar", 6, 0, 1024)
-        add_c(9, 0)
+        copy_x("vector", 3, 2, 4)
+        early_sums(1, 1)
+        quantize_x(2, 2, 4)
+        quantize_q("pool", 2, 0, 2)
+        exponent(3)
+        add_c(4, 1)
+        make_q("pool", 2, 2, 4)
+        early_sums(1, 0)
+        invert_sum(2)
+        add_c(5, 1)
+        weigh_row(1)
+        row_max(4)
+        early_sums(2, 1)
+        make_gain(2)
         square_x(3, 2, 4)
-        add_c(11, 1)
-        quantize_rw(0, 0, 512)
-        quantize_y(1)
-        logits(11, 0)
-        column_sums(6, 0)
-        mean_pass(0, 0)
-        column_sums(6, 1)
-        normalise("scalar", 7, 0, 1024)
-        quantize_xq(3, 0, 2)
-        logits(12, 1)
-        logits(13, 1)
-        row_max(9)
+        add_c(5, 0)
+        logits(6, 1)
+        invert_sum(3)
+        quantize_x(3, 2, 4)
+        logits(7, 0)
+        quantize_q("pool", 2, 2, 4)
+        exponent(4)
+        row_max(5)
+        make_q("pool", 3, 0, 2)
+        logits(7, 1)
+        early_sums(2, 0)
+        make_gain(3)
+        group_y("scalar", 1, 256, 512)
+        add_c(6, 0)
+        add_c(6, 1)
+        logits(8, 0)
+        invert_sum(4)
+        exponent(5)
+        add_c(7, 1)
+        logits(8, 1)
+        quantize_y("scalar", 0, 256, 512)
+        early_sums(3, 1)
+        quantize_x(3, 0, 2)
+        make_gain(4)
+        quantize_q("pool", 3, 0, 2)
+        weigh_row(3)
+        invert_sum(5)
+        add_c(7, 0)
         make_q("pool", 3, 2, 4)
-        invert_sum(8)
+        logits(9, 1)
+        add_c(8, 1)
+        make_gain(5)
+        weigh_row(2)
+        logits(9, 0)
+        add_c(8, 0)
+        logits(10, 1)
+        row_max(6)
+        weigh_row(0)
+        logits(10, 0)
+        early_sums(3, 0)
+        quantize_y("scalar", 1, 256, 512)
+        weigh_row(4)
+        quantize_q("pool", 3, 2, 4)
+        row_max(7)
+        group_rw("pool", 0, 256, 512)
+        early_sums(4, 1)
+        exponent(6)
+        row_max(8)
+        early_sums(4, 0)
+        exponent(7)
+        group_rw("vector", 0, 0, 256)
+        early_sums(5, 0)
+        quantize_rw("pool", 0, 256, 512)
+        exponent(8)
+        invert_sum(6)
+        add_c(9, 0)
+        group_rw("pool", 0, 512, 768)
+        early_sums(6, 0)
+        invert_sum(7)
+        add_c(9, 1)
+        make_gain(6)
+        weigh_row(5)
+        add_c(10, 1)
+        logits(11, 0)
         add_c(10, 0)
+        make_gain(7)
+        logits(11, 1)
+        weigh_row(6)
+        quantize_rw("pool", 0, 512, 768)
         add_c(11, 0)
-        weigh("pool", 1, 0, 256)
-        column_sums(7, 0)
-        group_y("scalar", 3, 0, 512)
-        row_max(10)
-        exponent(9)
-        column_sums(7, 1)
-        row_max(11)
-        normalise("scalar", 8, 0, 1024)
+        logits(12, 1)
+        group_rw("pool", 0, 768, 1024)
+        add_c(11, 1)
+        weigh_row(7)
         logits(12, 0)
-        add_c(12, 0)
+        row_max(9)
+        early_sums(7, 0)
+        group_y("scalar", 1, 0, 256)
+        quantize_rw("pool", 0, 768, 1024)
+        logits(13, 1)
+        row_max(10)
+        group_rw("pool", 1, 0, 256)
         logits(13, 0)
-        column_sums(8, 0)
-        invert_sum(9)
-        weigh("vector", 1, 256, 512)
-        quantize_xq(3, 2, 4)
+        copy_early("scalar", 0)
+        load_y(3)
+        early_sums(5, 1)
+        exponent(9)
+        row_max(11)
+        column_sums(7, 0)
         exponent(10)
+        quantize_rw("pool", 1, 0, 256)
+        invert_sum(8)
+        add_c(12, 1)
+        early_sums(6, 1)
+        group_rw("pool", 1, 256, 512)
+        add_c(12, 0)
         exponent(11)
         invert_sum(10)
-        normalise("scalar", 9, 0, 1024)
-        add_c(13, 1)
-        normalise("scalar", 10, 0, 1024)
-        column_sums(8, 1)
-        weigh("pool", 1, 512, 768)
-        logits(14, 0)
-        weigh("pool", 1, 768, 1024)
-        logits(15, 1)
-        add_c(12, 1)
-        column_sums(9, 0)
         add_c(13, 0)
-        column_sums(9, 1)
-        group_y("scalar", 2, 0, 512)
-        logits(14, 1)
+        early_sums(7, 1)
+        quantize_rw("vector", 0, 0, 256)
+        normalise("scalar", 8, 0, 1024)
+        quantize_rw("pool", 1, 256, 512)
+        logits(14, 0)
+        add_c(13, 1)
+        group_rw("pool", 1, 512, 768)
         row_max(12)
-        row_max(13)
+        logits(14, 1)
+        copy_early("scalar", 1)
+        column_sums(8, 0)
+        group_y("scalar", 2, 256, 512)
+        column_sums(7, 1)
         add_c(14, 0)
-        invert_sum(11)
-        column_sums(10, 0)
-        column_sums(10, 1)
-        normalise("pool", 11, 0, 1024)
-        add_c(14, 1)
-        row_max(14)
-        quantize_rw(1, 0, 512)
-        exponent(13)
-        quantize_rw(1, 512, 1024)
-        quantize_y(3)
+        column_sums(8, 1)
+        quantize_y("scalar", 1, 0, 256)
+        mean_pass(0, 0)
         exponent(12)
+        quantize_rw("pool", 1, 512, 768)
+        logits(15, 1)
+        invert_sum(11)
+        add_c(14, 1)
+        group_rw("pool", 1, 768, 1024)
         logits(15, 0)
-        column_sums(11, 1)
-        invert_sum(12)
-        add_c(15, 0)
-        add_c(15, 1)
-        exponent(14)
-        column_sums(11, 0)
-        weigh("pool", 2, 0, 256)
+        invert_sum(9)
+        row_max(13)
+        normalise("scalar", 10, 0, 1024)
         mean_pass(1, 0)
-        normalise("scalar", 12, 0, 1024)
         mean_pass(2, 0)
-        invert_sum(13)
-        mean_pass(1, 1)
-        invert_sum(14)
-        row_max(15)
+        mean_pass(0, 1)
+        invert_sum(12)
+        normalise("vector", 9, 0, 1024)
         mean_pass(3, 0)
-        column_sums(12, 1)
-        quantize_rw(0, 512, 1024)
-        weigh("vector", 2, 256, 512)
-        column_sums(12, 0)
-        normalise("scalar", 13, 0, 1024)
-        exponent(15)
-        invert_sum(15)
-        quantize_y(2)
-        normalise("scalar", 14, 0, 1024)
+        normalise("scalar", 11, 0, 1024)
+        mean_pass(3, 1)
+        quantize_rw("pool", 1, 768, 1024)
         mean_pass(2, 1)
-        normalise("scalar", 15, 0, 1024)
+        add_c(15, 1)
+        column_sums(9, 1)
+        normalise("scalar", 12, 0, 1024)
+        column_sums(9, 0)
+        add_c(15, 0)
+        weigh("pool", 2, 0, 256)
+        column_sums(10, 0)
+        row_max(14)
+        column_sums(10, 1)
+        exponent(13)
+        column_sums(11, 0)
+        column_sums(11, 1)
+        column_sums(12, 1)
+        row_max(15)
+        column_sums(12, 0)
+        exponent(14)
+        mean_pass(4, 0)
+        invert_sum(13)
+        weigh("vector", 2, 512, 768)
+        normalise("scalar", 13, 0, 1024)
+        mean_pass(4, 1)
+        invert_sum(14)
+        weigh("vector", 2, 256, 512)
+        exponent(15)
         column_sums(13, 1)
-        mean_pass(5, 0)
         column_sums(13, 0)
         weigh("vector", 2, 768, 1024)
-        quantize_rw(2, 0, 512)
-        mean_pass(3, 1)
-        mean_pass(0, 1)
-        mean_pass(4, 0)
+        mean_pass(5, 0)
+        normalise("scalar", 14, 0, 1024)
+        mean_pass(1, 1)
+        invert_sum(15)
+        quantize_rw("pool", 2, 0, 256)
+        group_y("scalar", 2, 0, 256)
+        normalise("vector", 15, 0, 1024)
         column_sums(14, 1)
+        quantize_y("scalar", 2, 256, 512)
         column_sums(14, 0)
-        column_sums(15, 0)
         weigh("vector", 3, 0, 256)
-        finish_nk(0)
-        mean_pass(1, 2)
-        quantize_rw(3, 0, 256)
-        invert_nk(0)
-        mean_pass(3, 2)
-        mean_pass(4, 1)
-        mean_pass(0, 2)
-        mean_pass(1, 3)
-        mean_pass(0, 3)
-        weigh("vector", 3, 256, 512)
-        mean_pass(6, 0)
-        weigh("vector", 2, 512, 768)
+        column_sums(15, 0)
+        group_y("scalar", 3, 0, 256)
         column_sums(15, 1)
-        quantize_rw(3, 256, 512)
         mean_pass(5, 1)
-        quantize_rw(2, 512, 1024)
-        mean_pass(6, 1)
+        quantize_y("scalar", 2, 0, 256)
+        quantize_rw("vector", 2, 256, 512)
+        group_y("scalar", 3, 256, 512)
+        mean_pass(1, 2)
+        quantize_rw("vector", 2, 768, 1024)
+        finish_nk(0)
+        mean_pass(0, 2)
+        quantize_rw("vector", 3, 0, 256)
+        mean_pass(3, 2)
+        invert_nk(0)
+        quantize_y("scalar", 3, 0, 256)
+        quantize_y("scalar", 3, 256, 512)
+        mean_pass(6, 0)
+        weigh("vector", 3, 256, 512)
+        mean_pass(0, 3)
+        mean_pass(1, 3)
         mean_pass(2, 2)
-        weigh("vector", 3, 512, 768)
-        divide("scalar", 1)
         divide("scalar", 0)
-        round_mean("scalar", 1)
-        finish_nk(1)
-        mean_pass(2, 3)
-        turn_mean(1)
-        mean_pass(3, 3)
-        store_mean(0)
-        round_mean("scalar", 0)
-        divide("scalar", 2)
-        copy_mean("scalar", 1)
-        round_mean("scalar", 2)
-        turn_mean(0)
-        mean_pass(4, 2)
-        mean_pass(5, 2)
-        quantize_rw(3, 512, 768)
+        quantize_rw("vector", 2, 512, 768)
+        mean_pass(6, 1)
+        quantize_rw("vector", 3, 256, 512)
+        divide("scalar", 1)
         mean_pass(6, 2)
-        weigh("vector", 3, 768, 1024)
-        mean_pass(4, 3)
+        weigh("vector", 3, 512, 768)
+        store_mean(0)
+        mean_pass(5, 2)
+        round_mean("scalar", 0)
+        mean_pass(3, 3)
         store_mean(1)
-        copy_mean("scalar", 0)
-        store_mean(2)
-        divide("scalar", 3)
-        mean_pass(7, 0)
+        mean_pass(2, 3)
+        round_mean("scalar", 1)
+        mean_pass(4, 2)
+        finish_nk(1)
+        turn_mean(0)
+        divide("scalar", 2)
+        quantize_rw("vector", 3, 512, 768)
+        turn_mean(1)
         invert_nk(1)
-        mean_pass(5, 3)
-        quantize_rw(3, 768, 1024)
+        mean_pass(7, 0)
+        divide("scalar", 3)
+        weigh("vector", 3, 768, 1024)
+        store_mean(2)
+        mean_pass(4, 3)
+        round_mean("scalar", 2)
         mean_pass(7, 1)
-        divide("vector", 4)
-        mean_pass(7, 2)
-        round_mean("scalar", 3)
-        quantize_p(0, 256)
-        mean_pass(7, 3)
-        mean_pass(6, 3)
-        divide("vector", 7)
-        turn_mean(3)
-        round_mean("vector", 4)
-        round_mean("vector", 7)
-        divide("scalar", 5)
-        turn_mean(2)
         store_mean(3)
-        round_mean("scalar", 5)
-        turn_mean(5)
+        mean_pass(5, 3)
+        divide("scalar", 4)
+        mean_pass(7, 2)
+        quantize_rw("vector", 3, 768, 1024)
+        round_mean("vector", 3)
+        divide("scalar", 5)
+        mean_pass(6, 3)
         store_mean(4)
+        round_mean("vector", 4)
+        copy_mean("scalar", 1)
+        mean_pass(7, 3)
+        round_mean("vector", 5)
         store_mean(5)
-        turn_mean(4)
+        turn_mean(3)
         divide("scalar", 6)
+        divide("vector", 7)
+        turn_mean(2)
+        turn_mean(5)
+        copy_mean("scalar", 3)
         round_mean("vector", 6)
-        copy_mean("scalar", 2)
-        turn_mean(7)
-        copy_mean("scalar", 5)
-        store_codes(0, 256)
-        store_mean(7)
-        copy_mean("vector", 3)
-        copy_mean("scalar", 4)
-        copy_mean("vector", 7)
-        quantize_p(256, 512)
-        quantize_p(512, 768)
         store_mean(6)
-        store_codes(256, 512)
-        store_codes(512, 768)
+        turn_mean(4)
+        copy_mean("scalar", 0)
+        store_mean(7)
+        round_mean("vector", 7)
+        copy_mean("scalar", 2)
         turn_mean(6)
+        copy_mean("vector", 4)
+        copy_mean("scalar", 5)
+        turn_mean(7)
+        quantize_p(0, 256)
         copy_mean("scalar", 6)
+        quantize_p(256, 512)
+        copy_mean("scalar", 7)
+        store_codes(0, 256)
+        quantize_p(512, 768)
+        store_codes(256, 512)
         quantize_p(768, 1024)
+        store_codes(512, 768)
         store_plane()
         store_codes(768, 1024)

@@ -24,7 +24,8 @@ BANK = 512
 KT = K // P
 RING = 4
 RUN = 2
-EARLY = 2 * PACK
+MID = range(PACK, 3 * PACK)
+FOLD = TILES
 
 
 def tile_quadraticsoftmaxweightedaverage_kernel(
@@ -98,9 +99,9 @@ def tile_quadraticsoftmaxweightedaverage_kernel(
         def rows_of(src, gi):
             return src[P * PACK * gi : P * PACK * (gi + 1), :].rearrange("(p t) d -> p t d", t=PACK)
 
-        def load_plane(plane, scales):
+        def load_plane(queue, plane, scales):
             for q in range(4):
-                nc.scalar.dma_start(
+                queue.dma_start(
                     out=plane[32 * q : 32 * q + 4, :].bitcast(I32), in_=scales[0, 4 * q : 4 * q + 4, :].bitcast(I32)
                 )
 
@@ -179,8 +180,8 @@ def tile_quadraticsoftmaxweightedaverage_kernel(
                 accum_out=row_sum[:, i : i + 1],
             )
 
-        def invert_sum(i):
-            nc.vector.reciprocal(out=inv_sum[:, i : i + 1], in_=row_sum[:, i : i + 1])
+        def invert_sum(i0, i1):
+            nc.vector.reciprocal(out=inv_sum[:, i0:i1], in_=row_sum[:, i0:i1])
 
         def normalise(engine, i, k0, k1):
             row = resp[i // PACK % 2][:, i % PACK, k0:k1]
@@ -219,41 +220,44 @@ def tile_quadraticsoftmaxweightedaverage_kernel(
 
         def early_sums(i, half):
             nc.tensor.matmul(
-                out=nk_banks[half][:],
+                out=turn_banks[half][:],
                 lhsT=inv_sum[:, i : i + 1].to_broadcast([P, P]),
                 rhs=resp[i // PACK % 2][:, i % PACK, BANK * half : BANK * (half + 1)],
-                start=(i == 0),
-                stop=(i == EARLY - 1),
+                start=(i == MID[0]),
+                stop=(i == MID[-1]),
             )
 
         def copy_early(engine, half):
             dst = early_nk[:, BANK * half : BANK * (half + 1)]
             if engine == "vector":
-                nc.vector.tensor_scalar(out=dst, in0=nk_banks[half][:], scalar1=1.0 / P, scalar2=None, op0=ALU.mult)
+                nc.vector.tensor_scalar(out=dst, in0=turn_banks[half][:], scalar1=1.0 / P, scalar2=None, op0=ALU.mult)
             else:
-                nc.scalar.activation(out=dst, in_=nk_banks[half][:], func=ACT.Copy, scale=1.0 / P)
+                nc.scalar.activation(out=dst, in_=turn_banks[half][:], func=ACT.Copy, scale=1.0 / P)
 
         def column_sums(i, half):
-            src = early_nk[:] if i == EARLY - 1 else resp[i // PACK % 2][:, i % PACK, :]
+            src = early_nk[:] if i == FOLD else resp[i // PACK % 2][:, i % PACK, :]
             for q in range(PACK):
                 kt = PACK * half + q
                 nc.tensor.matmul(
                     out=nk_banks[half][:, P * q : P * (q + 1)],
                     lhsT=src[:, P * kt : P * (kt + 1)],
                     rhs=ident[:],
-                    start=(i == EARLY - 1 and q == 0),
+                    start=(i == 0 and q == 0),
                     stop=(i == TILES - 1 and q == PACK - 1),
                     is_transpose=True,
                 )
 
         def interleave(engine, dst, src):
-            src = src.rearrange("p t n -> p n t")
             if engine == "pool":
-                nc.gpsimd.tensor_scalar(out=dst, in0=src, scalar1=1.0, scalar2=0.0, op0=ALU.mult, op1=ALU.add)
-            elif engine == "scalar":
-                nc.scalar.copy(out=dst, in_=src)
+                nc.gpsimd.tensor_scalar(
+                    out=dst, in0=src.rearrange("p t n -> p n t"), scalar1=1.0, scalar2=0.0, op0=ALU.mult, op1=ALU.add
+                )
             else:
-                nc.vector.tensor_copy(out=dst, in_=src)
+                move(
+                    engine,
+                    dst.rearrange("p (c i) t -> p c t i", i=PACK),
+                    src.rearrange("p t (c i) -> p c t i", i=PACK),
+                )
 
         def quantize_rw(engine, gi, k0, k1):
             quantize(rw_codes[gi][:, k0:k1], rw_plane[gi][:, k0:k1], staged(engine, rw_grouped[gi % 2][:, k0:k1, :]))
@@ -276,13 +280,23 @@ def tile_quadraticsoftmaxweightedaverage_kernel(
                 stop=(gi == GROUPS - 1),
             )
 
-        def finish_nk(half):
-            nc.vector.tensor_reduce(
-                out=nk[:, PACK * half : PACK * (half + 1)],
-                in_=nk_banks[half][:].rearrange("p (k i) -> p k i", i=P),
-                axis=mybir.AxisListType.X,
-                op=ALU.add,
-            )
+        def finish_nk(engine, half):
+            if engine == "vector":
+                nc.vector.tensor_reduce(
+                    out=nk[:, PACK * half : PACK * (half + 1)],
+                    in_=nk_banks[half][:].rearrange("p (k i) -> p k i", i=P),
+                    axis=mybir.AxisListType.X,
+                    op=ALU.add,
+                )
+            else:
+                for q in range(PACK):
+                    kt = PACK * half + q
+                    nc.scalar.activation(
+                        out=early_nk[:, P * kt : P * (kt + 1)],
+                        in_=nk_banks[half][:, P * q : P * (q + 1)],
+                        func=ACT.Copy,
+                        accum_out=nk[:, kt : kt + 1],
+                    )
 
         def divide(engine, kt):
             if engine == "vector":
@@ -338,7 +352,7 @@ def tile_quadraticsoftmaxweightedaverage_kernel(
             nc.vector.memset((eta_plane, dp_plane)[s][:].bitcast(U32), 0)
 
         def load_scales(s):
-            load_plane((eta_plane, dp_plane)[s], (eta_scales, dp_scales)[s])
+            load_plane((nc.scalar, nc.sync)[s], (eta_plane, dp_plane)[s], (eta_scales, dp_scales)[s])
 
         def clear_c():
             nc.vector.memset(c_row[:], 0.0)
@@ -379,387 +393,373 @@ def tile_quadraticsoftmaxweightedaverage_kernel(
 
         load_x(0, 0, 1)
         identity()
-        load_w()
         load_x(0, 1, 4)
         load_weight(1)
-        clear_plane(0)
         load_g()
-        clear_plane(1)
-        load_scales(0)
-        clear_c()
         clear_warm()
+        clear_c()
         warm_table()
         load_c()
-        turn_x(0, 0, 1)
-        load_x(1, 0, 4)
-        load_weight(0)
-        copy_x("vector", 0, 0, 1)
-        turn_x(0, 1, 2)
-        load_y(0)
-        square_x(0, 0, 1)
-        halve_g()
-        quantize_x(0, 0, 1)
-        turn_x(0, 2, 4)
+        clear_plane(1)
+        clear_plane(0)
         load_scales(1)
-        copy_x("vector", 0, 1, 2)
-        make_q("vector", 0, 0, 1)
-        square_x(0, 1, 2)
+        load_x(1, 0, 4)
+        turn_x(0, 0, 1)
+        load_weight(0)
+        load_scales(0)
+        copy_x("vector", 0, 0, 1)
+        turn_x(0, 2, 4)
+        load_w()
+        halve_g()
+        load_y(0)
+        quantize_x(0, 0, 1)
+        square_x(0, 0, 1)
+        turn_x(0, 1, 2)
+        copy_x("vector", 0, 2, 4)
         spread_c(0)
+        copy_x("scalar", 0, 1, 2)
+        make_q("vector", 0, 0, 1)
         load_x(2, 0, 4)
-        load_y(1)
-        quantize_q("vector", 0, 0, 1)
-        copy_x("scalar", 0, 2, 4)
-        quantize_x(0, 1, 2)
-        make_q("vector", 0, 1, 2)
-        spread_c(1)
-        square_x(0, 2, 4)
         turn_x(1, 0, 2)
-        copy_c("vector", 0)
-        quantize_q("vector", 0, 1, 2)
-        logits(1, 0)
+        square_x(0, 1, 2)
+        quantize_x(0, 1, 2)
+        load_y(1)
         quantize_x(0, 2, 4)
-        copy_c("vector", 1)
+        quantize_q("vector", 0, 0, 1)
+        square_x(0, 2, 4)
+        copy_c("vector", 0)
+        spread_c(1)
+        make_q("vector", 0, 1, 2)
         group_y("scalar", 0, 0, 256)
-        make_q("pool", 0, 2, 4)
         logits(0, 0)
         copy_x("vector", 1, 0, 2)
-        logits(0, 1)
-        add_c(1, 0)
-        group_y("scalar", 0, 256, 512)
-        turn_x(1, 2, 4)
-        add_c(0, 0)
-        turn_x(2, 0, 2)
-        add_c(0, 1)
-        load_x(3, 0, 4)
+        make_q("pool", 0, 2, 4)
+        copy_c("vector", 1)
         square_x(1, 0, 2)
-        logits(1, 1)
-        load_y(2)
-        quantize_y("scalar", 0, 0, 256)
-        quantize_x(1, 0, 2)
+        logits(0, 1)
+        add_c(0, 0)
+        turn_x(1, 2, 4)
+        add_c(0, 1)
+        group_y("scalar", 0, 256, 512)
+        load_x(3, 0, 4)
+        quantize_q("vector", 0, 1, 2)
+        logits(1, 0)
         quantize_q("pool", 0, 2, 4)
-        logits(2, 1)
-        copy_x("scalar", 1, 2, 4)
         row_max(0)
         make_q("pool", 1, 0, 2)
-        copy_x("scalar", 2, 0, 2)
+        copy_x("scalar", 1, 2, 4)
+        logits(1, 1)
+        load_y(2)
         logits(2, 0)
         square_x(1, 2, 4)
-        add_c(2, 1)
-        logits(3, 0)
-        add_c(2, 0)
-        turn_x(2, 2, 4)
-        exponent(0)
+        add_c(1, 0)
+        turn_x(2, 0, 2)
         add_c(1, 1)
-        turn_x(3, 0, 2)
-        quantize_x(1, 2, 4)
-        logits(3, 1)
+        exponent(0)
+        turn_x(2, 2, 4)
+        add_c(2, 0)
+        logits(3, 0)
+        quantize_x(1, 0, 4)
+        copy_x("scalar", 2, 0, 2)
+        logits(2, 1)
         quantize_q("pool", 1, 0, 2)
-        copy_x("scalar", 2, 2, 4)
         row_max(1)
+        copy_x("scalar", 2, 2, 4)
         make_q("pool", 1, 2, 4)
-        logits(4, 0)
+        logits(3, 1)
         square_x(2, 0, 2)
-        logits(4, 1)
-        invert_sum(0)
-        add_c(3, 0)
+        turn_x(3, 0, 2)
+        add_c(2, 1)
         turn_x(3, 2, 4)
+        add_c(3, 0)
         exponent(1)
+        logits(4, 1)
         row_max(2)
-        early_sums(0, 1)
-        make_gain(0)
-        quantize_x(2, 0, 2)
-        copy_x("scalar", 3, 0, 2)
-        quantize_q("pool", 1, 2, 4)
-        early_sums(0, 0)
+        logits(5, 0)
         square_x(2, 2, 4)
+        logits(4, 0)
+        quantize_q("pool", 1, 2, 4)
+        invert_sum(0, 2)
         add_c(3, 1)
         make_q("pool", 2, 0, 2)
-        invert_sum(1)
-        add_c(4, 0)
-        logits(5, 1)
         exponent(2)
-        row_max(3)
-        logits(5, 0)
-        logits(6, 0)
-        make_gain(1)
-        square_x(3, 0, 2)
-        copy_x("vector", 3, 2, 4)
-        early_sums(1, 1)
-        quantize_x(2, 2, 4)
-        quantize_q("pool", 2, 0, 2)
-        exponent(3)
         add_c(4, 1)
-        make_q("pool", 2, 2, 4)
-        early_sums(1, 0)
-        invert_sum(2)
-        add_c(5, 1)
-        weigh_row(1)
-        row_max(4)
-        early_sums(2, 1)
-        make_gain(2)
-        square_x(3, 2, 4)
-        add_c(5, 0)
+        logits(5, 1)
+        row_max(3)
         logits(6, 1)
-        invert_sum(3)
-        quantize_x(3, 2, 4)
+        normalise("scalar", 0, 0, 1024)
+        add_c(5, 1)
+        copy_x("scalar", 3, 0, 2)
+        column_sums(0, 1)
+        quantize_x(2, 0, 4)
+        exponent(3)
+        column_sums(0, 0)
+        quantize_q("pool", 2, 0, 2)
+        logits(7, 1)
+        add_c(4, 0)
+        make_q("pool", 2, 2, 4)
+        normalise("scalar", 1, 0, 1024)
+        add_c(5, 0)
+        logits(6, 0)
+        invert_sum(2, 4)
+        row_max(4)
         logits(7, 0)
+        normalise("scalar", 2, 0, 1024)
+        column_sums(1, 0)
+        column_sums(1, 1)
+        add_c(6, 1)
+        normalise("scalar", 3, 0, 1024)
+        column_sums(2, 1)
+        add_c(6, 0)
+        column_sums(2, 0)
         quantize_q("pool", 2, 2, 4)
+        logits(8, 0)
         exponent(4)
         row_max(5)
-        make_q("pool", 3, 0, 2)
-        logits(7, 1)
-        early_sums(2, 0)
-        make_gain(3)
-        group_y("scalar", 1, 256, 512)
-        add_c(6, 0)
-        add_c(6, 1)
-        logits(8, 0)
-        invert_sum(4)
+        weigh("pool", 0, 256, 512)
+        column_sums(3, 0)
+        column_sums(3, 1)
+        copy_x("scalar", 3, 2, 4)
+        add_c(7, 0)
+        logits(8, 1)
         exponent(5)
         add_c(7, 1)
-        logits(8, 1)
-        quantize_y("scalar", 0, 256, 512)
-        early_sums(3, 1)
-        quantize_x(3, 0, 2)
-        make_gain(4)
-        quantize_q("pool", 3, 0, 2)
-        weigh_row(3)
-        invert_sum(5)
-        add_c(7, 0)
-        make_q("pool", 3, 2, 4)
+        logits(9, 0)
+        row_max(6)
         logits(9, 1)
+        square_x(3, 2, 4)
+        invert_sum(4, 6)
+        quantize_rw("pool", 0, 256, 512)
+        early_sums(4, 1)
         add_c(8, 1)
         make_gain(5)
-        weigh_row(2)
-        logits(9, 0)
-        add_c(8, 0)
-        logits(10, 1)
-        row_max(6)
-        weigh_row(0)
-        logits(10, 0)
-        early_sums(3, 0)
-        quantize_y("scalar", 1, 256, 512)
-        weigh_row(4)
-        quantize_q("pool", 3, 2, 4)
-        row_max(7)
-        group_rw("pool", 0, 256, 512)
-        early_sums(4, 1)
+        make_gain(4)
+        weigh("pool", 0, 0, 256)
         exponent(6)
-        row_max(8)
+        row_max(7)
         early_sums(4, 0)
-        exponent(7)
-        group_rw("vector", 0, 0, 256)
-        early_sums(5, 0)
-        quantize_rw("pool", 0, 256, 512)
-        exponent(8)
-        invert_sum(6)
+        group_y("scalar", 1, 256, 512)
+        add_c(8, 0)
+        early_sums(5, 1)
         add_c(9, 0)
-        group_rw("pool", 0, 512, 768)
-        early_sums(6, 0)
-        invert_sum(7)
+        exponent(7)
+        weigh("vector", 0, 768, 1024)
+        logits(10, 1)
+        group_y("scalar", 1, 0, 256)
+        logits(10, 0)
+        quantize_rw("pool", 0, 0, 256)
+        invert_sum(6, 8)
         add_c(9, 1)
-        make_gain(6)
-        weigh_row(5)
-        add_c(10, 1)
+        weigh("pool", 0, 512, 768)
         logits(11, 0)
-        add_c(10, 0)
+        make_gain(6)
         make_gain(7)
+        load_y(3)
+        row_max(8)
+        square_x(3, 0, 2)
         logits(11, 1)
+        early_sums(5, 0)
+        row_max(9)
         weigh_row(6)
+        early_sums(6, 0)
+        add_c(10, 0)
+        exponent(8)
+        quantize_x(3, 0, 4)
+        early_sums(6, 1)
         quantize_rw("pool", 0, 512, 768)
-        add_c(11, 0)
-        logits(12, 1)
-        group_rw("pool", 0, 768, 1024)
+        exponent(9)
+        add_c(10, 1)
+        make_q("pool", 3, 0, 2)
+        early_sums(7, 1)
         add_c(11, 1)
         weigh_row(7)
-        logits(12, 0)
-        row_max(9)
-        early_sums(7, 0)
-        group_y("scalar", 1, 0, 256)
-        quantize_rw("pool", 0, 768, 1024)
-        logits(13, 1)
         row_max(10)
-        group_rw("pool", 1, 0, 256)
-        logits(13, 0)
-        copy_early("scalar", 0)
-        load_y(3)
-        early_sums(5, 1)
-        exponent(9)
-        row_max(11)
-        column_sums(7, 0)
+        early_sums(7, 0)
+        weigh_row(5)
+        add_c(11, 0)
+        quantize_q("pool", 3, 0, 2)
+        logits(12, 1)
         exponent(10)
-        quantize_rw("pool", 1, 0, 256)
-        invert_sum(8)
+        invert_sum(8, 10)
+        row_max(11)
+        make_q("pool", 3, 2, 4)
+        logits(12, 0)
+        weigh_row(4)
+        logits(13, 1)
         add_c(12, 1)
-        early_sums(6, 1)
-        group_rw("pool", 1, 256, 512)
+        logits(13, 0)
         add_c(12, 0)
-        exponent(11)
-        invert_sum(10)
-        add_c(13, 0)
-        early_sums(7, 1)
-        quantize_rw("vector", 0, 0, 256)
-        normalise("scalar", 8, 0, 1024)
-        quantize_rw("pool", 1, 256, 512)
-        logits(14, 0)
+        make_gain(9)
+        make_gain(8)
+        early_sums(8, 0)
         add_c(13, 1)
-        group_rw("pool", 1, 512, 768)
+        exponent(11)
+        quantize_rw("vector", 0, 768, 1024)
+        quantize_q("pool", 3, 2, 4)
+        logits(15, 1)
+        group_rw("scalar", 1, 0, 256)
+        add_c(13, 0)
+        group_rw("pool", 1, 256, 512)
+        logits(14, 0)
+        invert_sum(10, 12)
         row_max(12)
         logits(14, 1)
-        copy_early("scalar", 1)
-        column_sums(8, 0)
-        group_y("scalar", 2, 256, 512)
-        column_sums(7, 1)
-        add_c(14, 0)
-        column_sums(8, 1)
-        quantize_y("scalar", 1, 0, 256)
-        mean_pass(0, 0)
-        exponent(12)
-        quantize_rw("pool", 1, 512, 768)
-        logits(15, 1)
-        invert_sum(11)
-        add_c(14, 1)
-        group_rw("pool", 1, 768, 1024)
+        make_gain(10)
+        make_gain(11)
+        weigh_row(9)
         logits(15, 0)
-        invert_sum(9)
         row_max(13)
-        normalise("scalar", 10, 0, 1024)
-        mean_pass(1, 0)
-        mean_pass(2, 0)
-        mean_pass(0, 1)
-        invert_sum(12)
-        normalise("vector", 9, 0, 1024)
-        mean_pass(3, 0)
-        normalise("scalar", 11, 0, 1024)
-        mean_pass(3, 1)
-        quantize_rw("pool", 1, 768, 1024)
-        mean_pass(2, 1)
-        add_c(15, 1)
-        column_sums(9, 1)
-        normalise("scalar", 12, 0, 1024)
-        column_sums(9, 0)
-        add_c(15, 0)
-        weigh("pool", 2, 0, 256)
-        column_sums(10, 0)
-        row_max(14)
-        column_sums(10, 1)
+        early_sums(8, 1)
+        exponent(12)
+        quantize_y("scalar", 0, 0, 512)
+        early_sums(9, 1)
+        group_y("vector", 2, 256, 512)
         exponent(13)
-        column_sums(11, 0)
-        column_sums(11, 1)
-        column_sums(12, 1)
+        quantize_rw("pool", 1, 256, 512)
+        add_c(14, 0)
+        early_sums(9, 0)
+        group_rw("pool", 1, 512, 768)
+        weigh_row(8)
+        add_c(14, 1)
+        invert_sum(12, 14)
+        early_sums(10, 1)
+        add_c(15, 1)
+        weigh_row(11)
+        row_max(14)
+        early_sums(11, 1)
+        weigh_row(10)
+        normalise("vector", 13, 0, 1024)
+        early_sums(10, 0)
+        add_c(15, 0)
+        normalise("scalar", 12, 0, 1024)
+        quantize_y("scalar", 1, 0, 512)
+        early_sums(11, 0)
+        quantize_rw("pool", 1, 512, 768)
+        copy_early("scalar", 1)
         row_max(15)
-        column_sums(12, 0)
+        group_rw("pool", 2, 512, 768)
         exponent(14)
-        mean_pass(4, 0)
-        invert_sum(13)
-        weigh("vector", 2, 512, 768)
-        normalise("scalar", 13, 0, 1024)
-        mean_pass(4, 1)
-        invert_sum(14)
-        weigh("vector", 2, 256, 512)
-        exponent(15)
-        column_sums(13, 1)
-        column_sums(13, 0)
-        weigh("vector", 2, 768, 1024)
         mean_pass(5, 0)
+        mean_pass(3, 0)
+        copy_early("vector", 0)
+        mean_pass(3, 1)
+        exponent(15)
+        mean_pass(2, 0)
+        invert_sum(14, 15)
+        column_sums(16, 1)
+        group_y("vector", 2, 0, 256)
+        column_sums(16, 0)
+        quantize_rw("scalar", 1, 0, 256)
         normalise("scalar", 14, 0, 1024)
-        mean_pass(1, 1)
-        invert_sum(15)
-        quantize_rw("pool", 2, 0, 256)
-        group_y("scalar", 2, 0, 256)
-        normalise("vector", 15, 0, 1024)
-        column_sums(14, 1)
-        quantize_y("scalar", 2, 256, 512)
-        column_sums(14, 0)
-        weigh("vector", 3, 0, 256)
-        column_sums(15, 0)
+        column_sums(12, 0)
+        group_y("vector", 3, 256, 512)
+        mean_pass(1, 0)
+        mean_pass(2, 1)
+        invert_sum(15, 16)
+        group_rw("vector", 2, 256, 512)
+        column_sums(13, 0)
         group_y("scalar", 3, 0, 256)
-        column_sums(15, 1)
-        mean_pass(5, 1)
-        quantize_y("scalar", 2, 0, 256)
+        column_sums(12, 1)
+        quantize_rw("pool", 2, 512, 768)
+        column_sums(14, 0)
+        quantize_y("scalar", 2, 0, 512)
+        mean_pass(0, 0)
+        normalise("scalar", 15, 0, 1024)
         quantize_rw("vector", 2, 256, 512)
-        group_y("scalar", 3, 256, 512)
-        mean_pass(1, 2)
-        quantize_rw("vector", 2, 768, 1024)
-        finish_nk(0)
-        mean_pass(0, 2)
-        quantize_rw("vector", 3, 0, 256)
-        mean_pass(3, 2)
-        invert_nk(0)
-        quantize_y("scalar", 3, 0, 256)
-        quantize_y("scalar", 3, 256, 512)
-        mean_pass(6, 0)
+        mean_pass(0, 1)
+        quantize_y("scalar", 3, 0, 512)
+        mean_pass(4, 0)
+        mean_pass(5, 1)
+        group_rw("scalar", 2, 0, 256)
+        mean_pass(1, 1)
+        weigh("vector", 3, 0, 256)
+        column_sums(13, 1)
+        column_sums(15, 0)
+        group_rw("scalar", 1, 768, 1024)
+        column_sums(14, 1)
         weigh("vector", 3, 256, 512)
-        mean_pass(0, 3)
-        mean_pass(1, 3)
-        mean_pass(2, 2)
-        divide("scalar", 0)
-        quantize_rw("vector", 2, 512, 768)
-        mean_pass(6, 1)
-        quantize_rw("vector", 3, 256, 512)
-        divide("scalar", 1)
-        mean_pass(6, 2)
-        weigh("vector", 3, 512, 768)
-        store_mean(0)
+        column_sums(15, 1)
         mean_pass(5, 2)
-        round_mean("scalar", 0)
-        mean_pass(3, 3)
-        store_mean(1)
-        mean_pass(2, 3)
-        round_mean("scalar", 1)
-        mean_pass(4, 2)
-        finish_nk(1)
-        turn_mean(0)
-        divide("scalar", 2)
-        quantize_rw("vector", 3, 512, 768)
-        turn_mean(1)
-        invert_nk(1)
+        mean_pass(2, 2)
+        finish_nk("vector", 0)
+        finish_nk("scalar", 1)
+        mean_pass(4, 1)
+        mean_pass(3, 2)
+        quantize_rw("vector", 3, 256, 512)
+        quantize_rw("vector", 3, 0, 256)
+        group_rw("scalar", 2, 768, 1024)
         mean_pass(7, 0)
+        invert_nk(0)
+        quantize_rw("scalar", 2, 0, 256)
+        mean_pass(3, 3)
+        weigh("vector", 3, 512, 768)
+        mean_pass(2, 3)
+        mean_pass(0, 2)
         divide("scalar", 3)
-        weigh("vector", 3, 768, 1024)
-        store_mean(2)
-        mean_pass(4, 3)
-        round_mean("scalar", 2)
-        mean_pass(7, 1)
+        mean_pass(6, 0)
+        mean_pass(0, 3)
+        quantize_rw("scalar", 1, 768, 1024)
+        divide("scalar", 2)
+        mean_pass(1, 2)
+        quantize_rw("vector", 3, 512, 768)
         store_mean(3)
+        mean_pass(1, 3)
+        weigh("vector", 3, 768, 1024)
+        round_mean("scalar", 3)
+        mean_pass(4, 2)
+        store_mean(2)
+        mean_pass(6, 1)
+        divide("scalar", 1)
+        mean_pass(4, 3)
         mean_pass(5, 3)
-        divide("scalar", 4)
-        mean_pass(7, 2)
+        quantize_rw("scalar", 2, 768, 1024)
+        divide("scalar", 0)
+        mean_pass(7, 1)
+        invert_nk(1)
+        store_mean(1)
         quantize_rw("vector", 3, 768, 1024)
-        round_mean("vector", 3)
+        mean_pass(7, 2)
         divide("scalar", 5)
+        round_mean("vector", 1)
+        mean_pass(6, 2)
+        store_mean(0)
+        round_mean("vector", 2)
         mean_pass(6, 3)
-        store_mean(4)
-        round_mean("vector", 4)
-        copy_mean("scalar", 1)
+        divide("scalar", 4)
+        round_mean("vector", 0)
         mean_pass(7, 3)
-        round_mean("vector", 5)
         store_mean(5)
-        turn_mean(3)
-        divide("scalar", 6)
-        divide("vector", 7)
+        divide("vector", 6)
+        turn_mean(1)
+        divide("scalar", 7)
+        store_mean(4)
         turn_mean(2)
-        turn_mean(5)
-        copy_mean("scalar", 3)
+        round_mean("vector", 5)
+        turn_mean(3)
+        copy_mean("scalar", 1)
         round_mean("vector", 6)
-        store_mean(6)
-        turn_mean(4)
-        copy_mean("scalar", 0)
+        turn_mean(0)
         store_mean(7)
-        round_mean("vector", 7)
         copy_mean("scalar", 2)
+        round_mean("vector", 7)
+        turn_mean(5)
+        store_mean(6)
         turn_mean(6)
-        copy_mean("vector", 4)
-        copy_mean("scalar", 5)
+        copy_mean("scalar", 3)
+        round_mean("vector", 4)
         turn_mean(7)
-        quantize_p(0, 256)
+        copy_mean("scalar", 0)
+        copy_mean("vector", 5)
+        turn_mean(4)
         copy_mean("scalar", 6)
         quantize_p(256, 512)
         copy_mean("scalar", 7)
-        store_codes(0, 256)
-        quantize_p(512, 768)
+        quantize_p(0, 256)
+        copy_mean("scalar", 4)
         store_codes(256, 512)
         quantize_p(768, 1024)
+        store_codes(0, 256)
+        quantize_p(512, 768)
+        store_codes(768, 1024)
         store_codes(512, 768)
         store_plane()
-        store_codes(768, 1024)

from contextlib import ExitStack

import concourse.mybir as mybir
from concourse.masks import make_identity

N, D, K = 2048, 512, 1024
FLOPS = 3 * 2 * N * D * K

F32 = mybir.dt.float32
BF16 = mybir.dt.bfloat16
U32 = mybir.dt.uint32
I32 = mybir.dt.int32
U8 = mybir.dt.uint8
FP8X4 = mybir.dt.float8_e4m3fn_x4
FP4X4 = mybir.dt.float4_e2m1fn_x4
ALU = mybir.AluOpType
ACT = mybir.ActivationFunctionType

P = 128
PACK = 4
GROUPS = N // (P * PACK)
TILES = GROUPS * PACK
BANK = 512
KT = K // P
RING = 4
RUN = 2
MID = range(PACK, 3 * PACK)
FOLD = TILES


def tile_quadraticsoftmaxweightedaverage_kernel(
    tc, x, y, eta_words, eta_scales, dp_words, dp_scales, g, c, w, out_0, out_1, out_2
):
    nc = tc.nc
    with ExitStack() as ctx:
        sb = ctx.enter_context(tc.tile_pool(name="sb", bufs=1))
        ps = ctx.enter_context(tc.psum_pool(name="ps", bufs=1))
        ctx.enter_context(tc.manual_schedule())

        def sbuf(name, shape, dtype):
            return sb.tile(shape, dtype, name=name, align_bytes=64)

        banks = [ps.tile([P, BANK], F32, name="bank%d" % b) for b in range(8)]
        logit_banks = [banks[0:2], banks[2:4]]
        turn_banks = banks[4:6]
        nk_banks = banks[6:8]
        mean_banks = [banks[b] for b in (4, 5, 0, 1, 2, 3, 6, 7)]

        ident = sbuf("ident", [P, P], F32)
        minus_ones = sbuf("minus_ones", [P, P], BF16)
        c_row = sbuf("c_row", [P, K], BF16)
        minus_c = sbuf("minus_c", [P, K], F32)
        g_raw = sbuf("g_raw", [P, PACK], BF16)
        g_half = sbuf("g_half", [P, PACK], F32)
        w_raw = sbuf("w_raw", [P, GROUPS, PACK], BF16)
        warm = sbuf("warm", [P, 1], F32)
        eta_codes = sbuf("eta_codes", [P, 2 * K], U8)
        dp_codes = sbuf("dp_codes", [P, 2 * K], U8)
        eta_plane = sbuf("eta_plane", [P, K], U8)
        dp_plane = sbuf("dp_plane", [P, K], U8)
        x_raw = [sbuf("x_raw%d" % i, [P, PACK, D], BF16) for i in range(2)]
        y_raw = [sbuf("y_raw%d" % i, [P, PACK, D], BF16) for i in range(2)]
        x_grouped = [sbuf("x_grouped%d" % i, [P, PACK, P, PACK], BF16) for i in range(2)]
        q_grouped = [sbuf("q_grouped%d" % i, [P, PACK, P, PACK], BF16) for i in range(2)]
        stage = sbuf("stage", [P, 4 * P, PACK], BF16)
        sq = [sbuf("sq%d" % i, [P, PACK, P, PACK], F32) for i in range(2)]
        x_codes = sbuf("x_codes", [P, N], U32)
        x_plane = sbuf("x_plane", [P, N], U8)
        q_codes = sbuf("q_codes", [P, N], U32)
        q_plane = sbuf("q_plane", [P, N], U8)
        y_grouped = [sbuf("y_grouped%d" % i, [P, D, PACK], BF16) for i in range(2)]
        y_codes = [sbuf("y_codes%d" % i, [P, D], U32) for i in range(GROUPS)]
        y_plane = [sbuf("y_plane%d" % i, [P, D], U8) for i in range(GROUPS)]
        neg_logits = [sbuf("neg_logits%d" % i, [P, K], F32) for i in range(3)]
        resp = [sbuf("resp%d" % i, [P, PACK, K], F32) for i in range(2)]
        neg_max = sbuf("neg_max", [P, TILES], F32)
        row_sum = sbuf("row_sum", [P, TILES], F32)
        inv_sum = sbuf("inv_sum", [P, TILES], F32)
        rw_grouped = [sbuf("rw_grouped%d" % i, [P, K, PACK], BF16) for i in range(2)]
        rw_codes = [sbuf("rw_codes%d" % i, [P, K], U32) for i in range(GROUPS)]
        rw_plane = [sbuf("rw_plane%d" % i, [P, K], U8) for i in range(GROUPS)]
        gain = sbuf("gain", [P, TILES], F32)
        rw_rows = [sbuf("rw_rows%d" % i, [P, PACK, K], BF16) for i in range(2)]
        early_nk = sbuf("early_nk", [P, K], F32)
        nk = sbuf("nk", [P, KT], F32)
        inv_nk = sbuf("inv_nk", [P, KT], F32)
        mean = [sbuf("mean%d" % i, [P, D], F32) for i in range(KT)]
        mean_bf = [sbuf("mean_bf%d" % i, [P, D], BF16) for i in range(RING)]
        p_grouped = sbuf("p_grouped", [P, K, PACK], BF16)
        p_codes = sbuf("p_codes", [P, K], U32)
        p_plane = sbuf("p_plane", [P, K], U8)

        def move(engine, dst, src):
            if engine == "vector":
                nc.vector.tensor_copy(out=dst, in_=src)
            else:
                nc.scalar.copy(out=dst, in_=src)

        def rows_of(src, gi):
            return src[P * PACK * gi : P * PACK * (gi + 1), :].rearrange("(p t) d -> p t d", t=PACK)

        def load_plane(queue, plane, scales):
            for q in range(4):
                queue.dma_start(
                    out=plane[32 * q : 32 * q + 4, :].bitcast(I32), in_=scales[0, 4 * q : 4 * q + 4, :].bitcast(I32)
                )

        def turn_x(gi, t0, t1):
            for t in range(t0, t1):
                words = x_raw[gi % 2][:, t, :].bitcast(F32)
                for u in range(2):
                    col = (2 * (t % 2) + u) * P
                    nc.tensor.transpose(turn_banks[t // 2][:, col : col + P], words[:, u : D // 2 : 2], ident[:])

        def copy_x(engine, gi, t0, t1):
            src = turn_banks[t0 // 2][:].rearrange("p (t u m) -> p t m u", t=2, u=2)[:, t0 % 2 : t0 % 2 + t1 - t0]
            dst = x_grouped[gi % 2][:, t0:t1].bitcast(F32)
            move(engine, dst, src)

        def square_x(gi, t0, t1):
            nc.scalar.activation(out=sq[gi % 2][:, t0:t1], in_=x_grouped[gi % 2][:, t0:t1], func=ACT.Square)

        def staged(engine, own):
            return stage[:, : own.shape[1], :] if engine == "pool" else own

        def quantize(codes, plane, grouped):
            nc.vector.quantize_mx(out=codes.bitcast(FP8X4), scales=plane, in_=grouped.rearrange("p n j -> p (n j)"))

        def q_rows(engine, gi, t0, t1):
            return staged(engine, q_grouped[gi % 2][:, t0:t1].rearrange("p t m j -> p (t m) j"))

        def make_q(engine, gi, t0, t1):
            (nc.gpsimd if engine == "pool" else nc.vector).tensor_tensor(
                out=q_rows(engine, gi, t0, t1),
                in0=sq[gi % 2][:, t0:t1].rearrange("p t m j -> p (t m) j"),
                in1=g_half[:].unsqueeze(1).to_broadcast([P, (t1 - t0) * P, PACK]),
                op=ALU.mult,
            )

        def quantize_x(gi, t0, t1):
            cols = slice(P * (PACK * gi + t0), P * (PACK * gi + t1))
            quantize(x_codes[:, cols], x_plane[:, cols], x_grouped[gi % 2][:, t0:t1].rearrange("p t m j -> p (t m) j"))

        def quantize_q(engine, gi, t0, t1):
            cols = slice(P * (PACK * gi + t0), P * (PACK * gi + t1))
            quantize(q_codes[:, cols], q_plane[:, cols], q_rows(engine, gi, t0, t1))

        def logits(i, h):
            cols = slice(P * i, P * (i + 1))
            products = ((x_codes, x_plane, eta_codes, eta_plane), (q_codes, q_plane, dp_codes, dp_plane))
            for s, (act_codes, act_plane, codes, plane) in enumerate(products):
                nc.tensor.matmul_mx(
                    out=logit_banks[i % 2][h][:],
                    lhsT=act_codes[:, cols].bitcast(FP8X4),
                    lhsT_scale=act_plane[:, cols],
                    rhs=codes[:, 2 * BANK * h : 2 * BANK * (h + 1)].bitcast(FP4X4),
                    rhs_scale=plane[:, BANK * h : BANK * (h + 1)],
                    start=(s == 0),
                    stop=(s == 1),
                )

        def add_c(i, h):
            cols = slice(BANK * h, BANK * (h + 1))
            nc.vector.tensor_tensor(
                out=neg_logits[i % 3][:, cols], in0=minus_c[:, cols], in1=logit_banks[i % 2][h][:], op=ALU.subtract
            )

        def row_max(i):
            nc.vector.tensor_reduce(
                out=neg_max[:, i : i + 1], in_=neg_logits[i % 3][:], axis=mybir.AxisListType.X, op=ALU.min
            )

        def exponent(i):
            nc.scalar.activation(
                out=resp[i // PACK % 2][:, i % PACK, :],
                in_=neg_logits[i % 3][:],
                func=ACT.Exp,
                bias=neg_max[:, i : i + 1],
                scale=-1.0,
                accum_out=row_sum[:, i : i + 1],
            )

        def invert_sum(i0, i1):
            nc.vector.reciprocal(out=inv_sum[:, i0:i1], in_=row_sum[:, i0:i1])

        def normalise(engine, i, k0, k1):
            row = resp[i // PACK % 2][:, i % PACK, k0:k1]
            if engine == "scalar":
                nc.scalar.activation(out=row, in_=row, func=ACT.Copy, scale=inv_sum[:, i : i + 1])
            elif engine == "pool":
                nc.gpsimd.tensor_scalar(
                    out=row, in0=row, scalar1=inv_sum[:, i : i + 1], scalar2=1.0, op0=ALU.mult, op1=ALU.mult
                )
            else:
                nc.vector.tensor_scalar(out=row, in0=row, scalar1=inv_sum[:, i : i + 1], scalar2=None, op0=ALU.mult)

        def weigh(engine, gi, k0, k1):
            run = 1 if engine == "pool" else RUN
            (nc.gpsimd if engine == "pool" else nc.vector).tensor_tensor(
                out=staged(engine, rw_grouped[gi % 2][:, k0:k1, :]).rearrange("p (c i) t -> p c t i", i=run),
                in0=resp[gi % 2][:, :, k0:k1].rearrange("p t (c i) -> p c t i", i=run),
                in1=w_raw[:, gi, :].unsqueeze(1).unsqueeze(3).to_broadcast([P, (k1 - k0) // run, PACK, run]),
                op=ALU.mult,
            )

        def make_gain(i):
            gi, t = divmod(i, PACK)
            nc.scalar.activation(
                out=gain[:, i : i + 1], in_=w_raw[:, gi, t : t + 1], func=ACT.Copy, scale=inv_sum[:, i : i + 1]
            )

        def weigh_row(i):
            gi, t = divmod(i, PACK)
            nc.scalar.activation(
                out=rw_rows[gi % 2][:, t, :], in_=resp[gi % 2][:, t, :], func=ACT.Copy, scale=gain[:, i : i + 1]
            )

        def group_rw(engine, gi, k0, k1):
            interleave(engine, staged(engine, rw_grouped[gi % 2][:, k0:k1, :]), rw_rows[gi % 2][:, :, k0:k1])

        def early_sums(i, half):
            nc.tensor.matmul(
                out=turn_banks[half][:],
                lhsT=inv_sum[:, i : i + 1].to_broadcast([P, P]),
                rhs=resp[i // PACK % 2][:, i % PACK, BANK * half : BANK * (half + 1)],
                start=(i == MID[0]),
                stop=(i == MID[-1]),
            )

        def copy_early(engine, half):
            dst = early_nk[:, BANK * half : BANK * (half + 1)]
            if engine == "vector":
                nc.vector.tensor_scalar(out=dst, in0=turn_banks[half][:], scalar1=1.0 / P, scalar2=None, op0=ALU.mult)
            else:
                nc.scalar.activation(out=dst, in_=turn_banks[half][:], func=ACT.Copy, scale=1.0 / P)

        def column_sums(i, half):
            src = early_nk[:] if i == FOLD else resp[i // PACK % 2][:, i % PACK, :]
            for q in range(PACK):
                kt = PACK * half + q
                nc.tensor.matmul(
                    out=nk_banks[half][:, P * q : P * (q + 1)],
                    lhsT=src[:, P * kt : P * (kt + 1)],
                    rhs=ident[:],
                    start=(i == 0 and q == 0),
                    stop=(i == TILES - 1 and q == PACK - 1),
                    is_transpose=True,
                )

        def interleave(engine, dst, src):
            if engine == "pool":
                nc.gpsimd.tensor_scalar(
                    out=dst, in0=src.rearrange("p t n -> p n t"), scalar1=1.0, scalar2=0.0, op0=ALU.mult, op1=ALU.add
                )
            else:
                move(
                    engine,
                    dst.rearrange("p (c i) t -> p c t i", i=PACK),
                    src.rearrange("p t (c i) -> p c t i", i=PACK),
                )

        def quantize_rw(engine, gi, k0, k1):
            quantize(rw_codes[gi][:, k0:k1], rw_plane[gi][:, k0:k1], staged(engine, rw_grouped[gi % 2][:, k0:k1, :]))

        def group_y(engine, gi, d0, d1):
            interleave(engine, staged(engine, y_grouped[gi % 2][:, d0:d1, :]), y_raw[gi % 2][:, :, d0:d1])

        def quantize_y(engine, gi, d0, d1):
            quantize(y_codes[gi][:, d0:d1], y_plane[gi][:, d0:d1], staged(engine, y_grouped[gi % 2][:, d0:d1, :]))

        def mean_pass(kt, gi):
            cols = slice(P * kt, P * (kt + 1))
            nc.tensor.matmul_mx(
                out=mean_banks[kt][:],
                lhsT=rw_codes[gi][:, cols].bitcast(FP8X4),
                lhsT_scale=rw_plane[gi][:, cols],
                rhs=y_codes[gi][:].bitcast(FP8X4),
                rhs_scale=y_plane[gi][:],
                start=(gi == 0),
                stop=(gi == GROUPS - 1),
            )

        def finish_nk(engine, half):
            if engine == "vector":
                nc.vector.tensor_reduce(
                    out=nk[:, PACK * half : PACK * (half + 1)],
                    in_=nk_banks[half][:].rearrange("p (k i) -> p k i", i=P),
                    axis=mybir.AxisListType.X,
                    op=ALU.add,
                )
            else:
                for q in range(PACK):
                    kt = PACK * half + q
                    nc.scalar.activation(
                        out=early_nk[:, P * kt : P * (kt + 1)],
                        in_=nk_banks[half][:, P * q : P * (q + 1)],
                        func=ACT.Copy,
                        accum_out=nk[:, kt : kt + 1],
                    )

        def divide(engine, kt):
            if engine == "vector":
                nc.vector.tensor_scalar(
                    out=mean[kt][:], in0=mean_banks[kt][:], scalar1=inv_nk[:, kt : kt + 1], scalar2=None, op0=ALU.mult
                )
            else:
                nc.scalar.activation(
                    out=mean[kt][:], in_=mean_banks[kt][:], func=ACT.Copy, scale=inv_nk[:, kt : kt + 1]
                )

        def store_mean(kt):
            nc.sync.dma_start(out=out_0[P * kt : P * (kt + 1), :], in_=mean[kt][:])

        def round_mean(engine, kt):
            move(engine, mean_bf[kt % RING][:], mean[kt][:])

        def turn_mean(kt):
            words = mean_bf[kt % RING][:].bitcast(F32)
            for u in range(2):
                nc.tensor.transpose(mean_banks[kt][:, P * u : P * (u + 1)], words[:, u : D // 2 : 2], ident[:])

        def copy_mean(engine, kt):
            move(
                engine,
                p_grouped[:, P * kt : P * (kt + 1), :].bitcast(F32),
                mean_banks[kt][:, : 2 * P].rearrange("p (u m) -> p m u", u=2),
            )

        def quantize_p(k0, k1):
            quantize(p_codes[:, k0:k1], p_plane[:, k0:k1], p_grouped[:, k0:k1, :])

        def store_codes(k0, k1):
            words = out_1[0].rearrange("p m t -> p (m t)").bitcast(I32)
            nc.sync.dma_start(out=words[:, k0:k1], in_=p_codes[:, k0:k1].bitcast(I32))

        def store_plane():
            for q in range(4):
                nc.scalar.dma_start(
                    out=out_2[0, 4 * q : 4 * q + 4, :].bitcast(I32), in_=p_plane[32 * q : 32 * q + 4, :].bitcast(I32)
                )

        def load_x(gi, t0, t1):
            nc.sync.dma_start(out=x_raw[gi % 2][:, t0:t1, :], in_=rows_of(x, gi)[:, t0:t1, :])

        def load_y(gi):
            nc.sync.dma_start(out=y_raw[gi % 2][:], in_=rows_of(y, gi))

        def load_weight(s):
            nc.sync.dma_start(out=(eta_codes, dp_codes)[s][:].bitcast(I32), in_=(eta_words, dp_words)[s][0].bitcast(I32))

        def clear_plane(s):
            nc.vector.memset((eta_plane, dp_plane)[s][:].bitcast(U32), 0)

        def load_scales(s):
            load_plane((nc.scalar, nc.sync)[s], (eta_plane, dp_plane)[s], (eta_scales, dp_scales)[s])

        def clear_c():
            nc.vector.memset(c_row[:], 0.0)
            nc.vector.memset(minus_ones[:], -1.0)

        def load_c():
            nc.sync.dma_start(out=c_row[0:1, :], in_=c.rearrange("(o k) -> o k", o=1))

        def identity():
            make_identity(nc, ident[:])

        def load_g():
            nc.gpsimd.dma_start(out=g_raw[:], in_=g.rearrange("(p j) -> p j", j=PACK))

        def load_w():
            nc.sync.dma_start(out=w_raw[:], in_=w.rearrange("(g p t) -> p g t", g=GROUPS, t=PACK))

        def halve_g():
            nc.gpsimd.tensor_scalar(out=g_half[:], in0=g_raw[:], scalar1=-0.5, scalar2=1.0, op0=ALU.mult, op1=ALU.mult)

        def clear_warm():
            nc.vector.memset(warm[:], 0.0)

        def warm_table():
            nc.scalar.activation(out=warm[:], in_=warm[:], func=ACT.Exp)

        def spread_c(h):
            nc.tensor.matmul(
                out=banks[6 + h][:], lhsT=minus_ones[:], rhs=c_row[:, BANK * h : BANK * (h + 1)], start=True, stop=True
            )

        def copy_c(engine, h):
            move(engine, minus_c[:, BANK * h : BANK * (h + 1)], banks[6 + h][:])

        def invert_nk(half):
            cols = slice(PACK * half, PACK * (half + 1))
            nc.vector.reciprocal(out=inv_nk[:, cols], in_=nk[:, cols])

        load_x(0, 0, 1)
        identity()
        load_x(0, 1, 4)
        load_weight(1)
        load_g()
        clear_warm()
        clear_c()
        warm_table()
        load_c()
        clear_plane(1)
        clear_plane(0)
        load_scales(1)
        load_x(1, 0, 4)
        turn_x(0, 0, 1)
        load_weight(0)
        load_scales(0)
        copy_x("vector", 0, 0, 1)
        turn_x(0, 2, 4)
        load_w()
        halve_g()
        load_y(0)
        quantize_x(0, 0, 1)
        square_x(0, 0, 1)
        turn_x(0, 1, 2)
        copy_x("vector", 0, 2, 4)
        spread_c(0)
        copy_x("scalar", 0, 1, 2)
        make_q("vector", 0, 0, 1)
        load_x(2, 0, 4)
        turn_x(1, 0, 2)
        square_x(0, 1, 2)
        quantize_x(0, 1, 2)
        load_y(1)
        quantize_x(0, 2, 4)
        quantize_q("vector", 0, 0, 1)
        square_x(0, 2, 4)
        copy_c("vector", 0)
        spread_c(1)
        make_q("vector", 0, 1, 2)
        group_y("scalar", 0, 0, 256)
        logits(0, 0)
        copy_x("vector", 1, 0, 2)
        make_q("pool", 0, 2, 4)
        copy_c("vector", 1)
        square_x(1, 0, 2)
        logits(0, 1)
        add_c(0, 0)
        turn_x(1, 2, 4)
        add_c(0, 1)
        group_y("scalar", 0, 256, 512)
        load_x(3, 0, 4)
        quantize_q("vector", 0, 1, 2)
        logits(1, 0)
        quantize_q("pool", 0, 2, 4)
        row_max(0)
        make_q("pool", 1, 0, 2)
        copy_x("scalar", 1, 2, 4)
        logits(1, 1)
        load_y(2)
        logits(2, 0)
        square_x(1, 2, 4)
        add_c(1, 0)
        turn_x(2, 0, 2)
        add_c(1, 1)
        exponent(0)
        turn_x(2, 2, 4)
        add_c(2, 0)
        logits(3, 0)
        quantize_x(1, 0, 4)
        copy_x("scalar", 2, 0, 2)
        logits(2, 1)
        quantize_q("pool", 1, 0, 2)
        row_max(1)
        copy_x("scalar", 2, 2, 4)
        make_q("pool", 1, 2, 4)
        logits(3, 1)
        square_x(2, 0, 2)
        turn_x(3, 0, 2)
        add_c(2, 1)
        turn_x(3, 2, 4)
        add_c(3, 0)
        exponent(1)
        logits(4, 1)
        row_max(2)
        logits(5, 0)
        square_x(2, 2, 4)
        logits(4, 0)
        quantize_q("pool", 1, 2, 4)
        invert_sum(0, 2)
        add_c(3, 1)
        make_q("pool", 2, 0, 2)
        exponent(2)
        add_c(4, 1)
        logits(5, 1)
        row_max(3)
        logits(6, 1)
        normalise("scalar", 0, 0, 1024)
        add_c(5, 1)
        copy_x("scalar", 3, 0, 2)
        column_sums(0, 1)
        quantize_x(2, 0, 4)
        exponent(3)
        column_sums(0, 0)
        quantize_q("pool", 2, 0, 2)
        logits(7, 1)
        add_c(4, 0)
        make_q("pool", 2, 2, 4)
        normalise("scalar", 1, 0, 1024)
        add_c(5, 0)
        logits(6, 0)
        invert_sum(2, 4)
        row_max(4)
        logits(7, 0)
        normalise("scalar", 2, 0, 1024)
        column_sums(1, 0)
        column_sums(1, 1)
        add_c(6, 1)
        normalise("scalar", 3, 0, 1024)
        column_sums(2, 1)
        add_c(6, 0)
        column_sums(2, 0)
        quantize_q("pool", 2, 2, 4)
        logits(8, 0)
        exponent(4)
        row_max(5)
        weigh("pool", 0, 256, 512)
        column_sums(3, 0)
        column_sums(3, 1)
        copy_x("scalar", 3, 2, 4)
        add_c(7, 0)
        logits(8, 1)
        exponent(5)
        add_c(7, 1)
        logits(9, 0)
        row_max(6)
        logits(9, 1)
        square_x(3, 2, 4)
        invert_sum(4, 6)
        quantize_rw("pool", 0, 256, 512)
        early_sums(4, 1)
        add_c(8, 1)
        make_gain(5)
        make_gain(4)
        weigh("pool", 0, 0, 256)
        exponent(6)
        row_max(7)
        early_sums(4, 0)
        group_y("scalar", 1, 256, 512)
        add_c(8, 0)
        early_sums(5, 1)
        add_c(9, 0)
        exponent(7)
        weigh("vector", 0, 768, 1024)
        logits(10, 1)
        group_y("scalar", 1, 0, 256)
        logits(10, 0)
        quantize_rw("pool", 0, 0, 256)
        invert_sum(6, 8)
        add_c(9, 1)
        weigh("pool", 0, 512, 768)
        logits(11, 0)
        make_gain(6)
        make_gain(7)
        load_y(3)
        row_max(8)
        square_x(3, 0, 2)
        logits(11, 1)
        early_sums(5, 0)
        row_max(9)
        weigh_row(6)
        early_sums(6, 0)
        add_c(10, 0)
        exponent(8)
        quantize_x(3, 0, 4)
        early_sums(6, 1)
        quantize_rw("pool", 0, 512, 768)
        exponent(9)
        add_c(10, 1)
        make_q("pool", 3, 0, 2)
        early_sums(7, 1)
        add_c(11, 1)
        weigh_row(7)
        row_max(10)
        early_sums(7, 0)
        weigh_row(5)
        add_c(11, 0)
        quantize_q("pool", 3, 0, 2)
        logits(12, 1)
        exponent(10)
        invert_sum(8, 10)
        row_max(11)
        make_q("pool", 3, 2, 4)
        logits(12, 0)
        weigh_row(4)
        logits(13, 1)
        add_c(12, 1)
        logits(13, 0)
        add_c(12, 0)
        make_gain(9)
        make_gain(8)
        early_sums(8, 0)
        add_c(13, 1)
        exponent(11)
        quantize_rw("vector", 0, 768, 1024)
        quantize_q("pool", 3, 2, 4)
        logits(15, 1)
        group_rw("scalar", 1, 0, 256)
        add_c(13, 0)
        group_rw("pool", 1, 256, 512)
        logits(14, 0)
        invert_sum(10, 12)
        row_max(12)
        logits(14, 1)
        make_gain(10)
        make_gain(11)
        weigh_row(9)
        logits(15, 0)
        row_max(13)
        early_sums(8, 1)
        exponent(12)
        quantize_y("scalar", 0, 0, 512)
        early_sums(9, 1)
        group_y("vector", 2, 256, 512)
        exponent(13)
        quantize_rw("pool", 1, 256, 512)
        add_c(14, 0)
        early_sums(9, 0)
        group_rw("pool", 1, 512, 768)
        weigh_row(8)
        add_c(14, 1)
        invert_sum(12, 14)
        early_sums(10, 1)
        add_c(15, 1)
        weigh_row(11)
        row_max(14)
        early_sums(11, 1)
        weigh_row(10)
        normalise("vector", 13, 0, 1024)
        early_sums(10, 0)
        add_c(15, 0)
        normalise("scalar", 12, 0, 1024)
        quantize_y("scalar", 1, 0, 512)
        early_sums(11, 0)
        quantize_rw("pool", 1, 512, 768)
        copy_early("scalar", 1)
        row_max(15)
        group_rw("pool", 2, 512, 768)
        exponent(14)
        mean_pass(5, 0)
        mean_pass(3, 0)
        copy_early("vector", 0)
        mean_pass(3, 1)
        exponent(15)
        mean_pass(2, 0)
        invert_sum(14, 15)
        column_sums(16, 1)
        group_y("vector", 2, 0, 256)
        column_sums(16, 0)
        quantize_rw("scalar", 1, 0, 256)
        normalise("scalar", 14, 0, 1024)
        column_sums(12, 0)
        group_y("vector", 3, 256, 512)
        mean_pass(1, 0)
        mean_pass(2, 1)
        invert_sum(15, 16)
        group_rw("vector", 2, 256, 512)
        column_sums(13, 0)
        group_y("scalar", 3, 0, 256)
        column_sums(12, 1)
        quantize_rw("pool", 2, 512, 768)
        column_sums(14, 0)
        quantize_y("scalar", 2, 0, 512)
        mean_pass(0, 0)
        normalise("scalar", 15, 0, 1024)
        quantize_rw("vector", 2, 256, 512)
        mean_pass(0, 1)
        quantize_y("scalar", 3, 0, 512)
        mean_pass(4, 0)
        mean_pass(5, 1)
        group_rw("scalar", 2, 0, 256)
        mean_pass(1, 1)
        weigh("vector", 3, 0, 256)
        column_sums(13, 1)
        column_sums(15, 0)
        group_rw("scalar", 1, 768, 1024)
        column_sums(14, 1)
        weigh("vector", 3, 256, 512)
        column_sums(15, 1)
        mean_pass(5, 2)
        mean_pass(2, 2)
        finish_nk("vector", 0)
        finish_nk("scalar", 1)
        mean_pass(4, 1)
        mean_pass(3, 2)
        quantize_rw("vector", 3, 256, 512)
        quantize_rw("vector", 3, 0, 256)
        group_rw("scalar", 2, 768, 1024)
        mean_pass(7, 0)
        invert_nk(0)
        quantize_rw("scalar", 2, 0, 256)
        mean_pass(3, 3)
        weigh("vector", 3, 512, 768)
        mean_pass(2, 3)
        mean_pass(0, 2)
        divide("scalar", 3)
        mean_pass(6, 0)
        mean_pass(0, 3)
        quantize_rw("scalar", 1, 768, 1024)
        divide("scalar", 2)
        mean_pass(1, 2)
        quantize_rw("vector", 3, 512, 768)
        store_mean(3)
        mean_pass(1, 3)
        weigh("vector", 3, 768, 1024)
        round_mean("scalar", 3)
        mean_pass(4, 2)
        store_mean(2)
        mean_pass(6, 1)
        divide("scalar", 1)
        mean_pass(4, 3)
        mean_pass(5, 3)
        quantize_rw("scalar", 2, 768, 1024)
        divide("scalar", 0)
        mean_pass(7, 1)
        invert_nk(1)
        store_mean(1)
        quantize_rw("vector", 3, 768, 1024)
        mean_pass(7, 2)
        divide("scalar", 5)
        round_mean("vector", 1)
        mean_pass(6, 2)
        store_mean(0)
        round_mean("vector", 2)
        mean_pass(6, 3)
        divide("scalar", 4)
        round_mean("vector", 0)
        mean_pass(7, 3)
        store_mean(5)
        divide("vector", 6)
        turn_mean(1)
        divide("scalar", 7)
        store_mean(4)
        turn_mean(2)
        round_mean("vector", 5)
        turn_mean(3)
        copy_mean("scalar", 1)
        round_mean("vector", 6)
        turn_mean(0)
        store_mean(7)
        copy_mean("scalar", 2)
        round_mean("vector", 7)
        turn_mean(5)
        store_mean(6)
        turn_mean(6)
        copy_mean("scalar", 3)
        round_mean("vector", 4)
        turn_mean(7)
        copy_mean("scalar", 0)
        copy_mean("vector", 5)
        turn_mean(4)
        copy_mean("scalar", 6)
        quantize_p(256, 512)
        copy_mean("scalar", 7)
        quantize_p(0, 256)
        copy_mean("scalar", 4)
        store_codes(256, 512)
        quantize_p(768, 1024)
        store_codes(0, 256)
        quantize_p(512, 768)
        store_codes(768, 1024)
        store_codes(512, 768)
        store_plane()
